import numpy as np, ml_dtypes
CORES = [6,15,38,47]
N = 4
BF = ml_dtypes.bfloat16
def gentries(a):
    return np.ascontiguousarray(a.reshape(8, 16, -1).transpose(0, 2, 1)).reshape(8, -1)
def gtable(e):
    e = np.asarray(e); return np.ascontiguousarray(e.reshape(8, -1, 16).transpose(0, 2, 1)).reshape(128, -1).astype(np.int32)
H, W, P = 64, 64, 4096
A, B, Q = 32, 32, 1024
SW = 1
def pack(F, U, S, J):
    return {"fr": np.ascontiguousarray(F).reshape(N, 128, P).astype(np.float32).astype(BF), "qu": np.ascontiguousarray(U).reshape(N, 128, Q).astype(np.float32).astype(BF),
            "st": np.stack([gtable(v) for v in S]), "ju": np.stack([gtable(v) for v in J])}
def jumps(rng):
    n = (N, 8, SW * Q)
    return np.where(rng.random(n) < 0.5, rng.integers(-2, 3, n) * W + rng.integers(-2, 3, n), rng.integers(1 - P, P, n))
def scene(rng):
    base = rng.integers(0, 16, (8, 16, H, W)); dy = np.add.accumulate(rng.integers(-1, 2, (N, 8)), axis=0); dx = np.add.accumulate(rng.integers(-1, 2, (N, 8)), axis=0)
    F = np.zeros((N, 8, 16, H, W), np.int64); U = np.zeros((N, 8, 16, A, B), np.int64); S = np.zeros((N, 8, Q), np.int64)
    for r in range(N):
        for g in range(8):
            F[r, g] = np.roll(base[g], (int(dy[r, g]), int(dx[r, g])), axis=(1, 2))
            yy = (rng.integers(0, H) + np.arange(A)) % H; xx = (rng.integers(0, W) + np.arange(B)) % W
            U[r, g] = base[g][:, yy][:, :, xx]
            S[r, g] = (((yy + dy[r, g]) % H)[:, None] * W + ((xx + dx[r, g]) % W)[None, :]).reshape(-1)
    F = np.where(rng.random(F.shape) < 0.1, rng.integers(0, 16, F.shape), F); U = np.where(rng.random(U.shape) < 0.2, rng.integers(0, 16, U.shape), U)
    S = np.where(rng.random(S.shape) < 0.1, S, rng.integers(0, P, S.shape))
    return F.reshape(N, 8, 16, P), U.reshape(N, 8, 16, Q), S, jumps(rng)
def setup_inputs(rng):
    return pack(*scene(rng))
def setup_inputs_ties(rng):
    pat = rng.integers(0, 16, (8, 13, 16)); g = np.arange(8)[None, :, None]
    sub = np.argsort(rng.random((N, 8, 12)), axis=-1)[..., :6]
    idx = np.take_along_axis(sub, rng.integers(0, 6, (N, 8, P)), axis=-1)
    F = pat[g, idx].transpose(0, 1, 3, 2); U = pat[g, rng.integers(0, 13, (N, 8, Q))].transpose(0, 1, 3, 2)
    return pack(F, U, rng.integers(0, P, (N, 8, Q)), jumps(rng))
def setup_inputs_edges(rng):
    F, U, S, J = scene(rng)
    S = rng.choice(np.array([0, 1, H - 2, H - 1]), S.shape) * W + rng.choice(np.array([0, 1, W - 2, W - 1]), S.shape)
    J = rng.choice(np.array([0, 1, -1, W, -W, W - 1, P - 1, 1 - P]), J.shape)
    return pack(F, U, S, J)
def setup_inputs_far(rng):
    F = 15 * rng.integers(0, 2, (N, 8, 16, P)); U = 15 * rng.integers(0, 2, (N, 8, 16, Q)); h = rng.integers(0, 8)
    F[:, h] = 15; U[:, h] = 0
    return pack(F, U, rng.integers(0, P, (N, 8, Q)), jumps(rng))
def setup_inputs_one(rng):
    F, U, S, J = scene(rng)
    S = np.zeros_like(S) + rng.integers(0, P, (N, 8, 1)); J = np.zeros_like(J) + rng.integers(1 - P, P, (N, 8, 1))
    J[rng.integers(0, N)] = 0; k = rng.integers(0, N); F[k] = F[k][:, :, :1]
    return pack(F, U, S, J)
def setup_inputs_spread(rng):
    def uneven(n):
        e = np.exp2(rng.integers(-2, 4, (N, 8, 1, n))); v = np.minimum(np.floor(16 * rng.random((N, 8, 16, n)) ** e), 15)
        return v * (rng.random((N, 8, 1, n)) > 0.0625)
    F = uneven(P); U = uneven(Q)
    S = np.minimum(np.floor(P * rng.random((N, 8, Q)) ** 3), P - 1).astype(np.int64); S[:, :, 5] = P - 1
    J = rng.integers(1 - P, P, (N, 8, SW * Q)); J[:, :, 0] = P - 1; J[:, :, 1] = 1 - P
    return pack(F, U, S, J)
def check_inputs(d):
    bad = []
    for nm in ("fr", "qu"):
        v = d[nm].astype(np.float32)
        if not (np.isfinite(v).all() and (v == np.floor(v)).all() and v.min() >= 0 and v.max() <= 15): bad.append(nm)
    if d["st"].min() < 0 or d["st"].max() > P - 1: bad.append("st")
    if d["ju"].min() < 1 - P or d["ju"].max() > P - 1: bad.append("ju")
    return bad
def sides(p, t):
    i = np.arange(Q)
    a = np.roll(p, 1, axis=1); b = np.roll(p, B, axis=1)
    return np.where(i % B > 0, a + (a % W < W - 1), p), np.where(i >= B, np.where(b + W < P, b + W, b), p)
def reference(fr, qu, st, ju):
    F = fr.astype(np.int32).reshape(N, 8, 16, P); U = qu.astype(np.int32).reshape(N, 8, 16, Q)
    yc = np.zeros((N, 128, Q // 16), np.float32); yf = np.zeros_like(yc); yp = np.zeros_like(yc)
    for r in range(N):
        p = gentries(st[r]).astype(np.int64)
        bc = np.full((8, Q), 1 << 20, np.int64); bf = np.zeros((8, Q), np.int64); bp = np.zeros((8, Q), np.int64)
        for s in range(N):
            k = (r + s) % N; J = gentries(ju[k]).astype(np.int64).reshape(8, SW, Q)
            for t in range(SW):
                one, two = sides(p, t)
                c = np.stack([p, one, two, np.minimum(np.maximum(p + J[:, t], 0), P - 1)], axis=1)
                v = np.take_along_axis(F[k], c.reshape(8, 1, 4 * Q), axis=2).reshape(8, 16, 4, Q) - U[r][:, :, None, :]
                e = np.sum(v * v, axis=1); w = np.argmin(e, axis=1)[:, None]
                p = np.take_along_axis(c, w, axis=1)[:, 0]; best = np.take_along_axis(e, w, axis=1)[:, 0]
            m = best < bc
            bc = np.where(m, best, bc); bf = np.where(m, k, bf); bp = np.where(m, p, bp)
        yc[r] = gtable(bc); yf[r] = gtable(bf); yp[r] = gtable(bp)
    return {"yc": yc, "yf": yf, "yp": yp}

@@ -1,0 +1,454 @@
+from concourse.bass import DstId, RemoteDMATransfer
+from concourse.mybir import dt, AluOpType, AxisListType, ActivationFunctionType
+
+ALU = AluOpType
+ACT = ActivationFunctionType
+P, Q, K, W = 4096, 1024, 64, 32
+FW = P + 2 * K
+NP = 4
+MID, BIG = 1800, 30000.0
+HALF = "float16"
+LOC = (0, 1, 2, 0)
+FO = [(s - LOC[s]) % 4 for s in range(4)]
+FD = [d for d in FO if d]
+UD = sorted(set(LOC) - {0})
+
+SCRATCH = {
+    "fa": ("sbuf", [128, FW], "bfloat16"), "fb": ("sbuf", [128, len(FD), FW], "bfloat16"),
+    "ua": ("sbuf", [128, 4, Q], "bfloat16"), "usq": ("sbuf", [128, Q], "bfloat16"),
+    "nk": ("sbuf", [128, 4, 8 * W], HALF),
+    "jraw": ("sbuf", [128, K], "int32"), "jint": ("sbuf", [128, 2 * K], "int32"),
+    "mi": ("sbuf", [128, 4, K], "int32"), "mo": ("sbuf", [128, 4, K], "int32"), "mh": ("sbuf", [128, 4, K], "int32"),
+    "xyi": ("sbuf", [128, 4, 2, K], "int32"), "xyb": ("sbuf", [128, 16, K + 2], "bfloat16"),
+    "off": ("sbuf", [128, 8, 4 * W], "uint16"), "plc": ("sbuf", [128, 8, 4 * W], HALF),
+    "dd": ("sbuf", [128, 8, Q], "bfloat16"), "gg": ("sbuf", [128, 8, Q], "bfloat16"),
+    "sqe": ("sbuf", [128, 8, Q], "bfloat16"), "sql": ("sbuf", [128, 8, Q], "bfloat16"),
+    "kec": ("sbuf", [128, 8, K], "float32"), "ab": ("sbuf", [128, 8, K], "int32"), "abc": ("sbuf", [128, 8, K], "int32"),
+    "bs": ("sbuf", [128, 8, W], "int32"),
+    "ones": ("sbuf", [128, 128], "bfloat16"), "eye": ("sbuf", [128, 128], "bfloat16"), "eye64": ("sbuf", [128, 128], "bfloat16"),
+    "eyem2": ("sbuf", [128, 128], "bfloat16"), "sh": ("sbuf", [128, 2, 128], "bfloat16"), "wr": ("sbuf", [128, 2, 128], "bfloat16"),
+    "eyeh": ("sbuf", [128, 128], HALF), "eyek": ("sbuf", [128, 128], HALF), "low": ("sbuf", [128, 128], HALF),
+    "blk": ("sbuf", [128, 16], "bfloat16"), "sel": ("sbuf", [128, 144], "bfloat16"),
+    "pen": ("sbuf", [128, 16], "float32"),
+    "ti": ("sbuf", [128, 12, K], "int32"), "tf": ("sbuf", [128, 12, K], "float32"),
+    "oc": ("sbuf", [128, K], "float32"), "of": ("sbuf", [128, K], "float32"), "op": ("sbuf", [128, K], "float32"),
+}
+for _h in range(2):
+    for _n in ("pb2", "pb3", "pck", "pkl"):
+        SCRATCH[_n + str(_h)] = ("psum", [128, 512], "float32")
+
+ROLES = {"xy": 2, "cv": 2, "cc": 4, "off": 1, "plc": 1, "g0": 1, "g1": 1, "g2": 1, "g3": 1, "s0": 1, "s1": 1, "b2": 1, "b3": 1,
+         "m2": 1, "m3": 1, "ke": 1, "kl": 1, "kc": 1, "ab": 1, "ac": 1, "bs": 1, "mm": 1}
+SEMAPHORES = ([r + "_" + str(h) for r in ROLES for h in range(2)]
+              + ["arr%d_%d" % (s, h) for s in (1, 2, 3) for h in range(2)]
+              + ["hp%d" % k for k in range(NP)] + ["t%d" % k for k in range(14)]
+              + [a + str(k) for a in ("au", "an", "afb", "amh") for k in range(4)]
+              + ["ldf", "ldu", "lds", "ldj", "sty", "sent",
+                 "c0", "c1", "c2", "c3", "c4", "c5", "c6", "c7", "c8", "c9", "j0", "j1", "us", "nu", "nk0", "nk1", "nk2"])
+
+
+def mask_of(engs):
+    m = 0
+    for e in engs:
+        m |= 1 << e
+    return m
+
+
+def helpers_of(T, topo, rank):
+    n, src, out = len(T.cores), T.cores[rank], {}
+    free = [x for x in topo.cores_of(src) if T.rank_of(x) is None]
+    free.sort(key=lambda x: topo.die(x) == topo.die(src))
+    need = lambda d: len([x for x in free if topo.may_write(x, T.cores[(rank - d) % n])])
+    for d in sorted(FD, key=need):
+        out[d] = [x for x in free if topo.may_write(x, T.cores[(rank - d) % n]) and x not in out.values()][0]
+    return [out[d] for d in FD]
+
+
+def near_engines(topo, src, near, far):
+    return [e for e in topo.engines(src, near) if e not in topo.engines(src, far)]
+
+
+def helper_program(g, core, T, topo, rank, j):
+    hs = helpers_of(T, topo, rank)
+    dst = T.cores[(rank - FD[j]) % len(T.cores)]
+    engs = topo.engines(core, dst)
+    src = T.cores[rank] if j == 0 else hs[j - 1]
+    w, sent = FW // NP, 0
+    for k in range(NP):
+        piece = T.fb[:, 0, k * w:(k + 1) * w]
+        g.wait_ge(T.sem["hp%d" % k], len(near_engines(topo, src, core, dst)))
+        rid, pid, _ = topo.addr(dst)
+        g.remote_dma(T.fb[:, j, k * w:(k + 1) * w], piece, T.sem["afb%d" % j], T.sem.sent, pid, rid, mask_of(engs))
+        sent += len(engs)
+        if j + 1 < len(hs):
+            near = near_engines(topo, core, hs[j + 1], dst)
+            rid, pid, _ = topo.addr(hs[j + 1])
+            g.remote_dma(piece, piece, T.sem["hp%d" % k], T.sem.sent, pid, rid, mask_of(near))
+            sent += len(near)
+    g.wait_ge(T.sem.sent, sent)
+
+
+def rank_program(g, core, T, topo):
+    rank = T.rank_of(core)
+    n = len(T.cores)
+    if rank is None:
+        for r in range(n):
+            hs = helpers_of(T, topo, r)
+            if core in hs:
+                helper_program(g, core, T, topo, r, hs.index(core))
+        return
+    V, S, PE, SY = g.vector, g.scalar, g.tensor, g.sync
+    Qs = {"V": V, "S": S, "PE": PE, "SY": SY, "G": g}
+    seen = {k: {} for k in Qs}
+    total = {}
+
+    def wait(q, *toks):
+        for name, val in toks:
+            if seen[q].get(name, 0) < val:
+                Qs[q].wait_ge(T.sem[name], val)
+                seen[q][name] = val
+
+    def inc(ins, name, k=1):
+        ins.then_inc(T.sem[name], k)
+        total[name] = total.get(name, 0) + k
+
+    def tok(role, s, h):
+        if role in ("xy", "cv") and h == 1:
+            return (role + "_0", ROLES[role]) if s == 0 else (role + "_1", s * ROLES[role])
+        return (role + "_" + str(h), (s + 1) * ROLES[role])
+
+    def rinc(ins, role, h):
+        inc(ins, role + "_" + str(h))
+
+    peer = lambda d: T.cores[(rank + d) % n]
+    NE = len(topo.engines(core, peer(1)))
+
+    def send(dst, out, in_, sem, engs=None):
+        rid, pid, _ = topo.addr(dst)
+        engs = engs or topo.engines(core, dst)
+        g.remote_dma(out, in_, T.sem[sem], T.sem.sent, pid, rid, mask_of(engs))
+        total["sent"] = total.get("sent", 0) + len(engs)
+
+    inc(SY.dma_start(T.ua[:, 0, :], T.qu[:]), "ldu", 16)
+    inc(SY.dma_start(T.fa[:, 0:P], T.fr[:]), "ldf", 16)
+    inc(S.dma_start(T.mi[:, 0, :], T.st[:]), "lds", 16)
+    inc(S.dma_start(T.jraw[:], T.ju[:]), "ldj", 16)
+
+    inc(V.memset(T.ones[:], 1.0), "c0")
+    inc(V.memset(T.wr[:], 0.0), "c1")
+    inc(V.memset(T.sel[:], 0.0), "c1")
+    inc(V.memset(T.sh[:, :, 0:1], 0.0), "c1")
+    inc(V.memset(T.xyb[:, :, 0:2], 0.0), "c1")
+    inc(V.memset(T.low[:, 0:K], 2048.0), "c7")
+    inc(V.memset(T.low[:, K:2 * K], 6144.0), "c7")
+    inc(V.memset(T.nk[:, 0, :], -float(MID)), "nk0")
+    wait("G", ("c0", 1))
+    inc(g.affine_select(T.eye[:], T.ones[:], [[-1, 128]], ALU.is_equal, 0.0, 0, 1), "c2")
+    inc(g.affine_select(T.blk[:, 0:8], T.ones[:, 0:8], [[-16, 8]], ALU.is_ge, 0.0, 0, 1), "c8")
+    wait("G", ("c8", 1))
+    inc(g.affine_select(T.blk[:, 8:16], T.blk[:, 0:8], [[16, 8]], ALU.is_ge, 0.0, 15, -1), "c3")
+    wait("S", ("c2", 1))
+    inc(S.activation(T.eye64[:], T.eye[:], ACT.Copy, scale=64.0), "c6")
+    inc(S.activation(T.eyem2[:], T.eye[:], ACT.Copy, scale=-2.0), "c6")
+    wait("V", ("c1", 4), ("c2", 1))
+    inc(V.tensor_reduce(T.pen[:, 0:1], T.eye[:, 15:128:16], AxisListType.X, ALU.add), "c4")
+    inc(V.tensor_reduce(T.pen[:, 4:5], T.eye[:, 0:128:16], AxisListType.X, ALU.add), "c4")
+    inc(V.tensor_copy(T.wr[:, 0, 0:128:16], T.eye[:, 15:128:16]), "c5")
+    inc(V.tensor_scalar(T.wr[:, 1, 0:128:16], T.eye[:, 15:128:16], 64.0, None, ALU.mult), "c5")
+    wait("V", ("c4", 2))
+    inc(V.tensor_scalar(T.pen[:, 8:9], T.pen[:, 0:1], -1.0, 1.0, ALU.mult, ALU.add), "c9")
+    inc(V.tensor_scalar(T.pen[:, 12:13], T.pen[:, 4:5], BIG, None, ALU.mult), "c9")
+    inc(V.tensor_copy(T.eyeh[:], T.eye[:]), "c7")
+    inc(V.tensor_scalar(T.eyek[:], T.eye[:], 8192.0, None, ALU.mult), "c7")
+    wait("V", ("c3", 1))
+    inc(V.tensor_scalar(T.sel[:, 15:143:16], T.blk[:, 8:16], 8192.0, None, ALU.mult), "c7")
+    wait("V", ("c9", 2), ("nk0", 1))
+    inc(V.tensor_scalar(T.sh[:, 0, 1:128], T.eye[:, 0:127], T.pen[:, 8:9], None, ALU.mult), "c5")
+    inc(V.tensor_scalar(T.sh[:, 1, 1:128], T.eye[:, 0:127], T.pen[:, 8:9], 64.0, ALU.mult, ALU.mult), "c5")
+    for h in range(2):
+        c = h * 4 * W + 2 * W
+        inc(V.tensor_scalar(T.nk[:, 0, c:c + W:2], T.ones[:, 0:W // 2], T.pen[:, 12:13], -float(MID), ALU.mult, ALU.add), "nk2")
+    inc(V.memset(T.nk[:, 0, W:W + 2], BIG), "nk2")
+    wait("S", ("ldu", 16))
+    inc(S.activation(T.usq[:], T.ua[:, 0, :], ACT.Square), "us")
+    wait("PE", ("us", 1), ("c7", 5), ("c1", 4))
+
+    def t_norms():
+        for r in range(16):
+            ins = PE.matmul(T.pkl1[:, 0:K], T.sel[:, 15 - r:143 - r], T.usq[:, r:Q:16], r == 0, r == 15)
+        inc(ins, "nu")
+
+    def table():
+        wait("V", ("nu", 1))
+        for h in range(2):
+            for c in (W, 3 * W):
+                a = 2 if (h == 0 and c == W) else 0
+                inc(V.tensor_scalar(T.nk[:, 0, h * 4 * W + c + a:h * 4 * W + c + W], T.pkl1[:, h * W + a:(h + 1) * W],
+                                    1.0 / 8192, -float(MID), ALU.mult, ALU.add), "nk1")
+
+    NKT = [("nk2", 3), ("nk1", 4)]
+    NN = NE // max(len(UD), 1)
+    u_tok = [("au%d" % d, NE) if d else ("ldu", 16) for d in LOC]
+    n_tok = [[("an%d" % d, NN)] if d else NKT for d in LOC]
+    f_tok = [("afb%d" % FD.index(d), NP * NE) if d else ("ldf", 16) for d in FO]
+    j_tok = [("afb%d" % FD.index(d), NP * NE) if d else ("j1", 1) for d in FO]
+    frame = lambda s, a, b: T.fb[:, FD.index(FO[s]), a:b] if FO[s] else T.fa[:, a:b]
+    hop = lambda s: (LOC[s] - LOC[s - 1]) % n
+
+    def state(s, h, a, b):
+        if s == 0:
+            return T.mi[:, 0, a:b], ("lds", 16)
+        if hop(s):
+            return T.mi[:, s, a:b], ("arr%d_%d" % (s, h), NE)
+        return T.mo[:, s - 1, a:b], tok("mm", s - 1, h)
+
+    def result(s):
+        if LOC[s] == 0:
+            return T.mo[:, s, :], [tok("mm", s, 0), tok("mm", s, 1)]
+        if LOC[s + 1] == 0:
+            return T.mi[:, s + 1, :], [("arr%d_%d" % (s + 1, h), NE) for h in range(2)]
+        return T.mh[:, s, :], [("amh%d" % s, NE)]
+
+    def v_split(s, h, a, b, between=None):
+        m, t = state(s, h, a, b)
+        wait("V", t)
+        rinc(V.tensor_scalar(T.xyi[:, s, 0, a:b], m, 63, None, ALU.bitwise_and), "xy", h)
+        rinc(V.tensor_scalar(T.xyi[:, s, 1, a:b], m, 6, 63, ALU.arith_shift_right, ALU.bitwise_and), "xy", h)
+        if between:
+            between()
+        wait("V", tok("xy", s, h))
+        src = T.xyi[:, s, :, a:b]
+        rinc(V.tensor_copy(T.xyb[:, 4 * s:4 * s + 2, 2 + a:2 + b], src), "cv", h)
+        rinc(V.tensor_scalar(T.xyb[:, 4 * s + 2:4 * s + 4, 2 + a:2 + b], src, 1.0, 63.0, ALU.add, ALU.min), "cv", h)
+
+    def v_jumps():
+        wait("V", ("ldj", 16))
+        inc(V.tensor_scalar(T.jint[:, 0:K], T.jraw[:], 6, None, ALU.arith_shift_right), "j0")
+        inc(V.tensor_scalar(T.jint[:, K:2 * K], T.jraw[:], 63, None, ALU.bitwise_and), "j0")
+
+    def v_off(s, h):
+        i = 2 * s + h
+        wait("V", tok("cc", s, h))
+        rinc(V.tensor_scalar(T.off[:, i, :], T["pck%d" % h][:, 0:4 * W], 0.0, float(P - 1), ALU.max, ALU.min), "off", h)
+
+    def v_plc(s, h):
+        i = 2 * s + h
+        wait("V", tok("off", s, h))
+        rinc(V.tensor_scalar(T.plc[:, i, :], T.off[:, i, :], -2048.0, None, ALU.add), "plc", h)
+
+    def v_main(s, h):
+        i = 2 * s + h
+        u = T.ua[:, LOC[s], 512 * h:512 * (h + 1)]
+        win = frame(s, 0, P)
+        wait("V", tok("off", s, h), f_tok[s], u_tok[s])
+        rinc(V.tensor_tensor(T.dd[:, i, 0:512], win.indirect(T.off[:, i, 0:W]), u, ALU.subtract), "g0", h)
+        rinc(V.tensor_tensor(T.dd[:, i, 512:Q], win.indirect(T.off[:, i, 2 * W:3 * W]), u, ALU.subtract), "g1", h)
+        wait("V", tok("b2", s, h))
+        rinc(V.tensor_tensor(T.sqe[:, i, 512:Q], T["pb2%d" % h][:], T.gg[:, i, 0:512], ALU.mult), "m2", h)
+        wait("V", tok("b3", s, h))
+        rinc(V.tensor_tensor(T.sql[:, i, 512:Q], T["pb3%d" % h][:], T.gg[:, i, 512:Q], ALU.mult), "m3", h)
+
+    def v_min(s, h):
+        i = 2 * s + h
+        wait("V", tok("kc", s, h), tok("kl", s, h))
+        rinc(V.tensor_tensor(T.ab[:, i, :], T["pkl%d" % h][:, 0:K], T.kec[:, i, :], ALU.min), "ab", h)
+        wait("V", tok("ab", s, h))
+        rinc(V.tensor_scalar(T.abc[:, i, :], T.ab[:, i, :], -4097, None, ALU.bitwise_and), "ac", h)
+        wait("V", tok("ac", s, h))
+        rinc(V.tensor_scalar(T.bs[:, i, :], T.abc[:, i, W:K], 4096.0, None, ALU.add), "bs", h)
+        wait("V", tok("bs", s, h))
+        rinc(V.tensor_tensor(T.mo[:, s, h * W:(h + 1) * W], T.abc[:, i, 0:W], T.bs[:, i, :], ALU.min), "mm", h)
+
+    fr = [float((rank + s) % n) for s in range(4)]
+    ti = lambda k: T.ti[:, k, :]
+    tf = lambda k: T.tf[:, k, :]
+
+    def best_a():
+        m, t = result(0)
+        wait("V", *t)
+        inc(V.tensor_scalar(ti(0), m, -8192, None, ALU.bitwise_and), "t0")
+        inc(V.tensor_scalar(ti(1), m, P - 1, None, ALU.bitwise_and), "t0")
+
+    def best_b():
+        m, t = result(1)
+        wait("V", ("t0", 2), *t)
+        inc(V.tensor_tensor(tf(0), m, ti(0), ALU.is_ge), "t1")
+        inc(V.tensor_tensor(ti(2), m, ti(0), ALU.min), "t1")
+        wait("V", ("t1", 2))
+        inc(V.tensor_scalar(ti(3), ti(2), -8192, None, ALU.bitwise_and), "t2")
+        inc(V.tensor_scalar(ti(4), ti(2), P - 1, None, ALU.bitwise_and), "t2")
+        inc(V.tensor_tensor(tf(1), tf(0), ti(1), ALU.mult), "t2")
+        inc(V.tensor_scalar(tf(2), tf(0), fr[0] - fr[1], fr[1] - fr[2], ALU.mult, ALU.add), "t2")
+        wait("V", ("t2", 4))
+        inc(V.tensor_tensor(tf(3), tf(1), ti(4), ALU.add), "t3")
+
+    def best_c():
+        m, t = result(2)
+        wait("V", ("t3", 1), *t)
+        inc(V.tensor_tensor(tf(4), m, ti(3), ALU.is_ge), "t4")
+        inc(V.tensor_tensor(ti(5), m, ti(3), ALU.min), "t4")
+        wait("V", ("t4", 2))
+        inc(V.tensor_scalar(ti(6), ti(5), -8192, None, ALU.bitwise_and), "t5")
+        inc(V.tensor_scalar(ti(7), ti(5), P - 1, None, ALU.bitwise_and), "t5")
+        inc(V.tensor_tensor(tf(5), tf(4), tf(3), ALU.mult), "t5")
+        inc(V.tensor_tensor(tf(6), tf(4), tf(2), ALU.mult), "t5")
+        wait("V", ("t5", 4))
+        inc(V.tensor_tensor(tf(7), tf(5), ti(7), ALU.add), "t6")
+        inc(V.tensor_scalar(tf(8), tf(6), fr[2] - fr[3], None, ALU.add), "t6")
+
+    def best_d():
+        m, t = result(3)
+        wait("V", ("t6", 2), *t)
+        inc(V.tensor_tensor(ti(8), m, ti(6), ALU.min), "t7")
+        inc(V.tensor_tensor(tf(9), m, ti(6), ALU.is_ge), "t8")
+        wait("V", ("t7", 1))
+        inc(V.tensor_scalar(ti(9), ti(8), 13, None, ALU.arith_shift_right), "t9")
+        inc(V.tensor_scalar(ti(10), ti(8), P - 1, None, ALU.bitwise_and), "t10")
+        wait("V", ("t8", 1))
+        inc(V.tensor_tensor(tf(10), tf(9), tf(7), ALU.mult), "t10")
+        inc(V.tensor_tensor(tf(11), tf(9), tf(8), ALU.mult), "t11")
+        wait("V", ("t9", 1))
+        inc(V.tensor_scalar(T.oc[:], ti(9), float(MID), None, ALU.add), "t12")
+        wait("V", ("t10", 2))
+        inc(V.tensor_tensor(T.op[:], tf(10), ti(10), ALU.add), "t13")
+        wait("S", ("t11", 1))
+        inc(S.activation(T.of[:], tf(11), ACT.Identity, bias=fr[3]), "t11")
+
+    v_split(0, 0, 0, K, v_jumps)
+    wait("V", ("j0", 2))
+    inc(V.tensor_copy(T.fa[:, P:FW], T.jint[:]), "j1")
+    v_off(0, 0)
+    v_off(0, 1)
+    v_plc(0, 0)
+    v_plc(0, 1)
+    table()
+    for s in range(4):
+        for h in range(2):
+            if s > 0:
+                v_off(s, h)
+                v_plc(s, h)
+            v_main(s, h)
+            ns, nh = (s, 1) if h == 0 else (s + 1, 0)
+            if (s, h) == (1, 0):
+                best_a()
+            if (s, h) == (2, 1):
+                best_b()
+            if (s, h) == (3, 1):
+                best_c()
+            if 0 < ns < 4:
+                v_split(ns, nh, nh * W, (nh + 1) * W)
+            v_min(s, h)
+
+    for s in range(4):
+        for h in range(2):
+            i = 2 * s + h
+            win = frame(s, 0, P)
+            wait("S", tok("off", s, h), f_tok[s])
+            rinc(S.activation(T.gg[:, i, 0:512], win.indirect(T.off[:, i, W:2 * W]), ACT.Copy), "g2", h)
+            rinc(S.activation(T.gg[:, i, 512:Q], win.indirect(T.off[:, i, 3 * W:4 * W]), ACT.Copy), "g3", h)
+            wait("S", tok("g0", s, h))
+            rinc(S.activation(T.sqe[:, i, 0:512], T.dd[:, i, 0:512], ACT.Square), "s0", h)
+            wait("S", tok("g1", s, h))
+            rinc(S.activation(T.sql[:, i, 0:512], T.dd[:, i, 512:Q], ACT.Square), "s1", h)
+            wait("S", tok("ke", s, h))
+            rinc(S.activation(T.kec[:, i, :], T["pck%d" % h][:, 128:128 + K], ACT.Copy), "kc", h)
+    best_d()
+
+    def t_cand(s, h):
+        wait("PE", tok("cv", s, h), ("c5", 4), ("c6", 2), ("c2", 1), j_tok[s])
+        if h == 1:
+            wait("PE", tok("cv", s, 0))
+        pl = lambda k, d: T.xyb[:, 4 * s + k, 2 + h * W - d:2 + (h + 1) * W - d]
+        jp = lambda k: frame(s, P + k * K + h * W, P + k * K + (h + 1) * W)
+        e1, e64 = T.eye[:], T.eye64[:]
+        groups = [[(e64, pl(1, 0)), (e1, pl(0, 0))],
+                  [(e64, pl(3, 2)), (e1, pl(0, 2))],
+                  [(T.sh[:, 1, :], pl(1, 0)), (T.sh[:, 0, :], pl(2, 0)), (T.wr[:, 1, :], pl(1, 1)), (T.wr[:, 0, :], pl(2, 1))],
+                  [(e64, pl(1, 0)), (e1, pl(0, 0)), (e64, jp(0)), (e1, jp(1))]]
+        for k, grp in enumerate(groups):
+            for j, (a, b) in enumerate(grp):
+                ins = PE.matmul(T["pck%d" % h][:, k * W:(k + 1) * W], a, b, j == 0, j == len(grp) - 1)
+            rinc(ins, "cc", h)
+
+    def t_main(s, h):
+        i = 2 * s + h
+        u = T.ua[:, LOC[s], 512 * h:512 * (h + 1)]
+        ke, kl = T["pck%d" % h][:, 128:128 + K], T["pkl%d" % h][:, 0:K]
+        b2, b3 = T["pb2%d" % h][:], T["pb3%d" % h][:]
+        wait("PE", u_tok[s])
+        PE.matmul(b2, T.eyem2[:], u, True, False)
+        PE.matmul(b3, T.eyem2[:], u, True, False)
+        wait("PE", tok("g2", s, h))
+        rinc(PE.matmul(b2, T.eye[:], T.gg[:, i, 0:512], False, True), "b2", h)
+        wait("PE", tok("plc", s, h), *n_tok[s])
+        for j, kk in enumerate((ke, kl)):
+            PE.matmul(kk, T.eyeh[:], T.plc[:, i, j * K:(j + 1) * K], True, False)
+            PE.matmul(kk, T.eyek[:], T.nk[:, LOC[s], h * 4 * W + j * K:h * 4 * W + (j + 1) * K], False, False)
+            PE.matmul(kk, T.eyeh[:], T.low[:, j * K:(j + 1) * K], False, False)
+        wait("PE", tok("g3", s, h))
+        rinc(PE.matmul(b3, T.eye[:], T.gg[:, i, 512:Q], False, True), "b3", h)
+        for kk, sq, a, b, role in ((ke, T.sqe, "s0", "m2", "ke"), (kl, T.sql, "s1", "m3", "kl")):
+            wait("PE", tok(a, s, h), tok(b, s, h))
+            for r in range(16):
+                ins = PE.matmul(kk, T.sel[:, 15 - r:143 - r], sq[:, i, r:Q:16], False, r == 15)
+            rinc(ins, role, h)
+
+    t_norms()
+    t_cand(0, 0)
+    t_cand(0, 1)
+    for s in range(4):
+        for h in range(2):
+            t_main(s, h)
+            ns, nh = (s, 1) if h == 0 else (s + 1, 0)
+            if 0 < ns < 4:
+                t_cand(ns, nh)
+
+    wait("G", ("ldu", 16))
+    for d in UD:
+        send(peer(d), T.ua[:, d, :], T.ua[:, 0, :], "au%d" % d)
+    if UD:
+        wait("G", *NKT)
+        trs = []
+        for j, d in enumerate(UD):
+            rid, pid, _ = topo.addr(peer(d))
+            engs = topo.engines(core, peer(d))[j * NN:(j + 1) * NN]
+            trs.append(RemoteDMATransfer(dst_ids=[DstId(rid=rid, pnc=pid)], dma_engine_mask=mask_of(engs),
+                                         remote_sem=T.sem["an%d" % d], src=T.nk[:, 0, :], dst=T.nk[:, d, :]))
+        g.remote_dma_fused(trs, local_sem=T.sem.sent)
+        total["sent"] += NN * len(UD)
+    hp = helpers_of(T, topo, rank)[0]
+    near = near_engines(topo, core, hp, peer(1))
+    w = FW // NP
+
+    def piece(k):
+        wait("G", ("ldf", 16))
+        if k == NP - 1:
+            wait("G", ("j1", 1))
+        send(hp, T.fb[:, 0, k * w:(k + 1) * w], T.fa[:, k * w:(k + 1) * w], "hp%d" % k, near)
+
+    early = NP // 2 if FO[1] == 0 and FO[2] == 0 else NP
+    for k in range(early):
+        piece(k)
+    for s in range(3):
+        for h in range(2):
+            if hop(s + 1):
+                wait("G", tok("mm", s, h))
+                send(peer(hop(s + 1)), T.mi[:, s + 1, h * W:(h + 1) * W], T.mo[:, s, h * W:(h + 1) * W], "arr%d_%d" % (s + 1, h))
+            if (s, h) == (0, 0):
+                for k in range(early, NP):
+                    piece(k)
+        if LOC[s] and LOC[s + 1]:
+            wait("G", tok("mm", s, 0), tok("mm", s, 1))
+            send(peer(-LOC[s]), T.mh[:, s, :], T.mo[:, s, :], "amh%d" % s)
+
+    wait("SY", ("t12", 1))
+    inc(SY.dma_start(T.yc[:], T.oc[:]), "sty", 16)
+    wait("S", ("t11", 2))
+    inc(S.dma_start(T.yf[:], T.of[:]), "sty", 16)
+    wait("SY", ("t13", 1))
+    inc(SY.dma_start(T.yp[:], T.op[:]), "sty", 16)
+    waited = {}
+    for q in seen:
+        for k, v in seen[q].items():
+            waited[k] = max(waited.get(k, 0), v)
+    wait("G", *[(k, v) for k, v in total.items() if waited.get(k, 0) < v])

@@ -1,50 +1,68 @@
-from concourse.bass import DstId, RemoteDMATransfer
 from concourse.mybir import dt, AluOpType, AxisListType, ActivationFunctionType
 
 ALU = AluOpType
 ACT = ActivationFunctionType
-P, Q, K, W = 4096, 1024, 64, 32
-FW = P + 2 * K
-NP = 4
-MID, BIG = 1800, 30000.0
+P, Q, K = 4096, 1024, 64
+CUT = (0, 32, 64)
+NH = len(CUT) - 1
+W = max(b - a for a, b in zip(CUT, CUT[1:]))
+NN = 4 * NH
+J = 2 * K
+MID, BIG = 1800, 4096.0
 HALF = "float16"
-LOC = (0, 1, 2, 0)
-FO = [(s - LOC[s]) % 4 for s in range(4)]
-FD = [d for d in FO if d]
-UD = sorted(set(LOC) - {0})
+GUEST = 1
+SLOT = (0, 0, 1, 2)
+ROUTES = ("VVMM", "VVMM", "VSVM", "VSVM")
+POS = (0, 2, 1, 3)
+
+LOADS = ("u", (0, P))
+FEEDS = ((1664, 2272, 0), (2272, 2880, 1), (2880, 3488, 0), (3488, P, 1))
+HELP = [[(a, b, s) for s in (2, 3) for a, b, x in FEEDS if x == h] for h in range(2)]
+OWN = {0: ((-J, 768, 2),), 1: ((768, 1664, 2),), 2: ((-J, 768, 3),), 3: ((768, 1664, 3),)}
+
+AWAY = {"V": [("g0", 0), ("plc", 0), ("g1", 0), ("s2", 0), ("s3", 0), ("xy", 1), ("cv", 1),
+              ("m1", 0), ("m2", 0), ("m3", 0), ("m4", 0), ("off", 1)],
+        "S": [("g2", 0), ("g3", 0), ("s0", 0), ("s1", 0), ("kc", 0)],
+        "PE": [("a2", 0), ("a3", 0), ("pre", 0), ("b2", 0), ("b3", 0), ("ke", 0), ("kl", 0), ("cc", 1)]}
+HOME = {"V": [("g0", 0), ("m1", -1), ("q2", -1), ("m2", -1), ("g2", 0), ("m3", -1), ("q3", -1), ("plc", 0), ("q4", -1),
+              ("q5", -1), ("m4", -1), ("xy", 1), ("q6", -1), ("cv", 1), ("s3", 0), ("q7", -1), ("q0", 0), ("off", 1), ("q1", 0)],
+        "S": [("g1", 0), ("g3", 0), ("s0", 0), ("s2", 0), ("s1", 0), ("kc", 0)],
+        "PE": [("a1", 0), ("b1", 0), ("a3", 0), ("b3", 0), ("pre", 0), ("cc", 1), ("ke", 0), ("kl", 0)]}
+BEST_AT = {2 * NH: 1, 3 * NH: 2}
 
 SCRATCH = {
-    "fa": ("sbuf", [128, FW], "bfloat16"), "fb": ("sbuf", [128, len(FD), FW], "bfloat16"),
-    "ua": ("sbuf", [128, 4, Q], "bfloat16"), "usq": ("sbuf", [128, Q], "bfloat16"),
-    "nk": ("sbuf", [128, 4, 8 * W], HALF),
+    "fa": ("sbuf", [128, 3, J + P], "bfloat16"),
+    "ua": ("sbuf", [128, 2, Q], "bfloat16"), "usq": ("sbuf", [128, Q], "bfloat16"),
+    "nq": ("sbuf", [128, 2, NH * 2 * W], HALF),
     "jraw": ("sbuf", [128, K], "int32"), "jint": ("sbuf", [128, 2 * K], "int32"),
-    "mi": ("sbuf", [128, 4, K], "int32"), "mo": ("sbuf", [128, 4, K], "int32"), "mh": ("sbuf", [128, 4, K], "int32"),
+    "mo": ("sbuf", [128, 5, K], "int32"), "mg": ("sbuf", [128, 2, K], "int32"),
     "xyi": ("sbuf", [128, 4, 2, K], "int32"), "xyb": ("sbuf", [128, 16, K + 2], "bfloat16"),
-    "off": ("sbuf", [128, 8, 4 * W], "uint16"), "plc": ("sbuf", [128, 8, 4 * W], HALF),
-    "dd": ("sbuf", [128, 8, Q], "bfloat16"), "gg": ("sbuf", [128, 8, Q], "bfloat16"),
-    "sqe": ("sbuf", [128, 8, Q], "bfloat16"), "sql": ("sbuf", [128, 8, Q], "bfloat16"),
-    "kec": ("sbuf", [128, 8, K], "float32"), "ab": ("sbuf", [128, 8, K], "int32"), "abc": ("sbuf", [128, 8, K], "int32"),
-    "bs": ("sbuf", [128, 8, W], "int32"),
+    "off": ("sbuf", [128, NN, 4 * W], "uint16"), "plc": ("sbuf", [128, NN, 4 * W], HALF),
+    "gd": ("sbuf", [128, NN, 64 * W], "bfloat16"), "sq": ("sbuf", [128, NN, 64 * W], "bfloat16"),
+    "kec": ("sbuf", [128, NN, 2 * W], "float32"), "ab": ("sbuf", [128, NN, 2 * W], "int32"),
+    "abc": ("sbuf", [128, NN, 2 * W], "int32"), "bs": ("sbuf", [128, NN, W], "int32"),
     "ones": ("sbuf", [128, 128], "bfloat16"), "eye": ("sbuf", [128, 128], "bfloat16"), "eye64": ("sbuf", [128, 128], "bfloat16"),
-    "eyem2": ("sbuf", [128, 128], "bfloat16"), "sh": ("sbuf", [128, 2, 128], "bfloat16"), "wr": ("sbuf", [128, 2, 128], "bfloat16"),
-    "eyeh": ("sbuf", [128, 128], HALF), "eyek": ("sbuf", [128, 128], HALF), "low": ("sbuf", [128, 128], HALF),
+    "eyem": ("sbuf", [128, 2, 128], "bfloat16"), "sh": ("sbuf", [128, 2, 128], "bfloat16"), "wr": ("sbuf", [128, 2, 128], "bfloat16"),
+    "eyeh": ("sbuf", [128, 128], HALF), "eyek": ("sbuf", [128, 128], HALF),
+    "cl": ("sbuf", [128, 128], "bfloat16"), "ct": ("sbuf", [128, 2 * NH, 2, 2 * W], "bfloat16"),
     "blk": ("sbuf", [128, 16], "bfloat16"), "sel": ("sbuf", [128, 144], "bfloat16"),
     "pen": ("sbuf", [128, 16], "float32"),
-    "ti": ("sbuf", [128, 12, K], "int32"), "tf": ("sbuf", [128, 12, K], "float32"),
+    "ti": ("sbuf", [128, 16, K], "int32"), "tf": ("sbuf", [128, 4, K], "float32"),
     "oc": ("sbuf", [128, K], "float32"), "of": ("sbuf", [128, K], "float32"), "op": ("sbuf", [128, K], "float32"),
 }
 for _h in range(2):
-    for _n in ("pb2", "pb3", "pck", "pkl"):
+    for _n in ("pa", "pb", "pc", "pl"):
         SCRATCH[_n + str(_h)] = ("psum", [128, 512], "float32")
+KE = 256
 
-ROLES = {"xy": 2, "cv": 2, "cc": 4, "off": 1, "plc": 1, "g0": 1, "g1": 1, "g2": 1, "g3": 1, "s0": 1, "s1": 1, "b2": 1, "b3": 1,
-         "m2": 1, "m3": 1, "ke": 1, "kl": 1, "kc": 1, "ab": 1, "ac": 1, "bs": 1, "mm": 1}
-SEMAPHORES = ([r + "_" + str(h) for r in ROLES for h in range(2)]
-              + ["arr%d_%d" % (s, h) for s in (1, 2, 3) for h in range(2)]
-              + ["hp%d" % k for k in range(NP)] + ["t%d" % k for k in range(14)]
-              + [a + str(k) for a in ("au", "an", "afb", "amh") for k in range(4)]
-              + ["ldf", "ldu", "lds", "ldj", "sty", "sent",
-                 "c0", "c1", "c2", "c3", "c4", "c5", "c6", "c7", "c8", "c9", "j0", "j1", "us", "nu", "nk0", "nk1", "nk2"])
+ROLES = {"xy": 2, "cv": 2, "cc": 4, "off": 1, "plc": 1, "g0": 1, "g1": 1, "g2": 1, "g3": 1, "s0": 1, "s1": 1, "s2": 1, "s3": 1,
+         "b1": 1, "b2": 1, "b3": 1, "ke": 1, "kl": 1, "kc": 1, "m1": 1, "m2": 1, "m3": 1, "m4": 1}
+FIN = {"fn": 1, "fk": 1, "fc": 1, "fp": 2, "ff": 1, "yc": 1, "yp": 1, "yf": 1}
+SEMAPHORES = ([r + "_" + str(h) for r in list(ROLES) + list(FIN) for h in range(NH)]
+              + ["ldf%d" % k for k in range(len(LOADS))] + ["hp%d" % k for k in range(len(FEEDS))]
+              + ["arr%d" % n for n in range(NH, 3 * NH)] + [a + str(k) for a in ("af", "aj") for k in (2, 3)]
+              + [a + str(k) for a in "tc" for k in range(12)]
+              + ["ldu", "lds", "ldj", "sty", "sent", "j0", "j1", "us", "nu", "nk", "au", "an"])
 
 
 def mask_of(engs):
@@ -55,45 +73,45 @@ def mask_of(engs):
 
 
 def helpers_of(T, topo, rank):
-    n, src, out = len(T.cores), T.cores[rank], {}
-    free = [x for x in topo.cores_of(src) if T.rank_of(x) is None]
-    free.sort(key=lambda x: topo.die(x) == topo.die(src))
-    need = lambda d: len([x for x in free if topo.may_write(x, T.cores[(rank - d) % n])])
-    for d in sorted(FD, key=need):
-        out[d] = [x for x in free if topo.may_write(x, T.cores[(rank - d) % n]) and x not in out.values()][0]
-    return [out[d] for d in FD]
+    me = T.cores[rank]
+    return sorted([x for x in topo.cores_of(me) if x != me and all(topo.may_write(x, c) for c in T.cores)],
+                  key=lambda x: topo.die(x) == topo.die(me))
 
 
-def near_engines(topo, src, near, far):
-    return [e for e in topo.engines(src, near) if e not in topo.engines(src, far)]
+def near_engines(T, topo, rank):
+    me = T.cores[rank]
+    return [e for e in topo.engines(me, helpers_of(T, topo, rank)[0]) if e not in topo.engines(me, T.cores[rank - 1])]
 
 
-def helper_program(g, core, T, topo, rank, j):
-    hs = helpers_of(T, topo, rank)
-    dst = T.cores[(rank - FD[j]) % len(T.cores)]
-    engs = topo.engines(core, dst)
-    src = T.cores[rank] if j == 0 else hs[j - 1]
-    w, sent = FW // NP, 0
-    for k in range(NP):
-        piece = T.fb[:, 0, k * w:(k + 1) * w]
-        g.wait_ge(T.sem["hp%d" % k], len(near_engines(topo, src, core, dst)))
-        rid, pid, _ = topo.addr(dst)
-        g.remote_dma(T.fb[:, j, k * w:(k + 1) * w], piece, T.sem["afb%d" % j], T.sem.sent, pid, rid, mask_of(engs))
-        sent += len(engs)
-        if j + 1 < len(hs):
-            near = near_engines(topo, core, hs[j + 1], dst)
-            rid, pid, _ = topo.addr(hs[j + 1])
-            g.remote_dma(piece, piece, T.sem["hp%d" % k], T.sem.sent, pid, rid, mask_of(near))
-            sent += len(near)
+def write(g, T, topo, dst, out, in_, sem, engs):
+    rid, pid, _ = topo.addr(dst)
+    g.remote_dma(out, in_, T.sem[sem], T.sem.sent, pid, rid, mask_of(engs))
+    return len(engs)
+
+
+def hand_on(g, core, T, topo, rank, a, b, s):
+    dst = T.cores[rank - s]
+    return write(g, T, topo, dst, T.fa[:, SLOT[s], J + a:J + b], T.fa[:, 0, J + a:J + b], ("aj%d" if a < 0 else "af%d") % s,
+                 topo.engines(core, dst))
+
+
+def helper_program(g, core, T, topo, rank, h):
+    sent, here = 0, []
+    for a, b, s in HELP[h]:
+        k = FEEDS.index((a, b, h))
+        if k not in here:
+            here.append(k)
+            g.wait_ge(T.sem["hp%d" % k], len(near_engines(T, topo, rank)))
+        sent += hand_on(g, core, T, topo, rank, a, b, s)
     g.wait_ge(T.sem.sent, sent)
 
 
 def rank_program(g, core, T, topo):
     rank = T.rank_of(core)
-    n = len(T.cores)
+    nr = len(T.cores)
     if rank is None:
-        for r in range(n):
-            hs = helpers_of(T, topo, r)
+        for r in range(nr):
+            hs = helpers_of(T, topo, r)[:len(HELP)]
             if core in hs:
                 helper_program(g, core, T, topo, r, hs.index(core))
         return
@@ -112,36 +130,32 @@ def rank_program(g, core, T, topo):
         ins.then_inc(T.sem[name], k)
         total[name] = total.get(name, 0) + k
 
-    def tok(role, s, h):
-        if role in ("xy", "cv") and h == 1:
-            return (role + "_0", ROLES[role]) if s == 0 else (role + "_1", s * ROLES[role])
-        return (role + "_" + str(h), (s + 1) * ROLES[role])
+    def tok(role, n):
+        return (role + "_" + str(n % NH), (n // NH + 1) * ROLES[role] if n >= 0 else 0)
 
-    def rinc(ins, role, h):
-        inc(ins, role + "_" + str(h))
+    def rinc(ins, role, n):
+        inc(ins, role + "_" + str(n % NH))
 
-    peer = lambda d: T.cores[(rank + d) % n]
+    peer = lambda d: T.cores[(rank + d) % nr]
     NE = len(topo.engines(core, peer(1)))
 
-    def send(dst, out, in_, sem, engs=None):
-        rid, pid, _ = topo.addr(dst)
-        engs = engs or topo.engines(core, dst)
-        g.remote_dma(out, in_, T.sem[sem], T.sem.sent, pid, rid, mask_of(engs))
-        total["sent"] = total.get("sent", 0) + len(engs)
-
-    inc(SY.dma_start(T.ua[:, 0, :], T.qu[:]), "ldu", 16)
-    inc(SY.dma_start(T.fa[:, 0:P], T.fr[:]), "ldf", 16)
-    inc(S.dma_start(T.mi[:, 0, :], T.st[:]), "lds", 16)
+    inc(S.dma_start(T.mo[:, 0, :], T.st[:]), "lds", 16)
     inc(S.dma_start(T.jraw[:], T.ju[:]), "ldj", 16)
+    for k, x in enumerate(LOADS):
+        if x == "u":
+            inc(SY.dma_start(T.ua[:, 0, :], T.qu[:]), "ldu", 16)
+        else:
+            inc(SY.dma_start(T.fa[:, 0, J + x[0]:J + x[1]], T.fr[:, x[0]:x[1]]), "ldf%d" % k, 16)
+    loaded = lambda a, b: [("ldf%d" % k, 16) for k, x in enumerate(LOADS) if x != "u" and x[0] < b and a < x[1]]
 
     inc(V.memset(T.ones[:], 1.0), "c0")
     inc(V.memset(T.wr[:], 0.0), "c1")
     inc(V.memset(T.sel[:], 0.0), "c1")
     inc(V.memset(T.sh[:, :, 0:1], 0.0), "c1")
     inc(V.memset(T.xyb[:, :, 0:2], 0.0), "c1")
-    inc(V.memset(T.low[:, 0:K], 2048.0), "c7")
-    inc(V.memset(T.low[:, K:2 * K], 6144.0), "c7")
-    inc(V.memset(T.nk[:, 0, :], -float(MID)), "nk0")
+    inc(V.memset(T.cl[:], 0.0), "c10")
+    inc(V.memset(T.ct[:], 0.0), "c10")
+    inc(V.memset(T.nq[:, 0, :], -float(MID)), "c10")
     wait("G", ("c0", 1))
     inc(g.affine_select(T.eye[:], T.ones[:], [[-1, 128]], ALU.is_equal, 0.0, 0, 1), "c2")
     inc(g.affine_select(T.blk[:, 0:8], T.ones[:, 0:8], [[-16, 8]], ALU.is_ge, 0.0, 0, 1), "c8")
@@ -149,304 +163,268 @@ def rank_program(g, core, T, topo):
     inc(g.affine_select(T.blk[:, 8:16], T.blk[:, 0:8], [[16, 8]], ALU.is_ge, 0.0, 15, -1), "c3")
     wait("S", ("c2", 1))
     inc(S.activation(T.eye64[:], T.eye[:], ACT.Copy, scale=64.0), "c6")
-    inc(S.activation(T.eyem2[:], T.eye[:], ACT.Copy, scale=-2.0), "c6")
+    inc(S.activation(T.eyem[:, 0, :], T.eye[:], ACT.Copy, scale=-1.0), "c6")
+    inc(S.activation(T.eyem[:, 1, :], T.eye[:], ACT.Copy, scale=-2.0), "c6")
+    wait("V", ("c10", 3))
+    inc(V.memset(T.cl[0:1, :], 8192.0), "c7")
+    inc(V.memset(T.cl[32:33, :], 2048.0), "c7")
+    inc(V.memset(T.cl[64:65, 0:128:16], 8192.0), "c7")
+    inc(V.memset(T.ct[0:1, NH:2 * NH, :, :], -float(MID)), "c11")
+    inc(V.memset(T.ct[32:33, :, 0, :], 1.0), "c7")
+    inc(V.memset(T.ct[32:33, :, 1, :], 3.0), "c7")
+    for h in range(NH):
+        inc(V.memset(T.ct[64:65, h:2 * NH:NH, 1, 0:CUT[h + 1] - CUT[h]:2], BIG), "c7")
+    wait("V", ("c11", 1))
+    inc(V.memset(T.ct[0:1, 0:2 * NH:NH, 0, CUT[1]:CUT[1] + 2], BIG), "c7")
     wait("V", ("c1", 4), ("c2", 1))
     inc(V.tensor_reduce(T.pen[:, 0:1], T.eye[:, 15:128:16], AxisListType.X, ALU.add), "c4")
-    inc(V.tensor_reduce(T.pen[:, 4:5], T.eye[:, 0:128:16], AxisListType.X, ALU.add), "c4")
     inc(V.tensor_copy(T.wr[:, 0, 0:128:16], T.eye[:, 15:128:16]), "c5")
     inc(V.tensor_scalar(T.wr[:, 1, 0:128:16], T.eye[:, 15:128:16], 64.0, None, ALU.mult), "c5")
-    wait("V", ("c4", 2))
+    wait("V", ("c4", 1))
     inc(V.tensor_scalar(T.pen[:, 8:9], T.pen[:, 0:1], -1.0, 1.0, ALU.mult, ALU.add), "c9")
-    inc(V.tensor_scalar(T.pen[:, 12:13], T.pen[:, 4:5], BIG, None, ALU.mult), "c9")
     inc(V.tensor_copy(T.eyeh[:], T.eye[:]), "c7")
     inc(V.tensor_scalar(T.eyek[:], T.eye[:], 8192.0, None, ALU.mult), "c7")
     wait("V", ("c3", 1))
     inc(V.tensor_scalar(T.sel[:, 15:143:16], T.blk[:, 8:16], 8192.0, None, ALU.mult), "c7")
-    wait("V", ("c9", 2), ("nk0", 1))
+    wait("V", ("c9", 1))
     inc(V.tensor_scalar(T.sh[:, 0, 1:128], T.eye[:, 0:127], T.pen[:, 8:9], None, ALU.mult), "c5")
     inc(V.tensor_scalar(T.sh[:, 1, 1:128], T.eye[:, 0:127], T.pen[:, 8:9], 64.0, ALU.mult, ALU.mult), "c5")
-    for h in range(2):
-        c = h * 4 * W + 2 * W
-        inc(V.tensor_scalar(T.nk[:, 0, c:c + W:2], T.ones[:, 0:W // 2], T.pen[:, 12:13], -float(MID), ALU.mult, ALU.add), "nk2")
-    inc(V.memset(T.nk[:, 0, W:W + 2], BIG), "nk2")
+    wait("PE", ("c7", total["c7"]), ("c1", 4), ("c5", 4), ("c6", 3), ("c2", 1))
+
+    far = [x for l in list(HELP) + list(OWN.values()) for x in l]
+    own_f, own_j = loaded(0, P), [("j1", 1)]
+    j_tok = [own_j, own_j] + [[("aj%d" % s, NE)] for s in (2, 3)]
+    f_tok = [own_f, own_f] + [[("af%d" % s, NE * len([x for x in far if x[2] == s and x[0] >= 0]))] + j_tok[s] for s in (2, 3)]
+    u_tok = lambda s: ("au", NE) if s == GUEST else ("ldu", 16)
+    n_tok = lambda s: ("an", NE) if s == GUEST else ("nk", NH)
+    span = lambda n: (n // NH, CUT[n % NH], CUT[n % NH + 1], CUT[n % NH + 1] - CUT[n % NH])
+    ps = lambda name, n: T[name + str(n % 2)]
+    through = lambda n: [c for c in range(4) if ROUTES[n // NH][c] != "V"]
+
+    def bank(c, n):
+        return "pb%d" % (n % 2) if c == 3 else "pa%d" % (n % 2 if len(through(n)) < 3 else c % 2)
+
+    formed = lambda c, n: ("b%d_%d" % (c, n % NH), len([m for m in range(n % NH, n + 1, NH) if c in through(m)]))
+    k_in = lambda s, a, b: T.mg[:, 0, a:b] if s == GUEST else T.mo[:, s, a:b]
+    k_out = lambda s, a, b: T.mg[:, 1, a:b] if s == GUEST else T.mo[:, s + 1, a:b]
+
+    def there(n):
+        s = n // NH
+        return ("lds", 16) if s == 0 else ("arr%d" % n, NE) if s in (GUEST, GUEST + 1) else tok("m4", n - NH)
+
+    last = float((rank + 3) % nr)
+    ti = lambda k: T.ti[:, k, :]
+
+    def best(s, j):
+        m = T.mo[:, s + 1, :]
+        k = 4 * s - 4
+        if j == 0:
+            wait("V", ("t2", s - 1), *[there((s + 1) * NH + h) for h in range(NH)])
+            inc(V.tensor_scalar(T.ti[:, k:k + 2, :], T.mo[:, s:s + 2, :], -4097, None, ALU.bitwise_and), "t%d" % k)
+            if s == 2:
+                inc(V.tensor_scalar(ti(3), T.mo[:, 2, :], 12, 1, ALU.arith_shift_right, ALU.bitwise_and), "t3")
+        elif j == 1:
+            wait("V", ("t%d" % k, 1))
+            inc(V.tensor_scalar(ti(k + 2), ti(k + 1), 4096.0, None, ALU.add), "t%d" % (k + 1))
+        elif j == 2:
+            wait("V", ("t%d" % (k + 1), 1), *[tok("xy", (s + 1) * NH + h) for h in range(NH)])
+            inc(V.tensor_tensor(m, ti(k), ti(k + 2), ALU.min), "t%d" % (k + 2))
+        elif s < 2:
+            return
+        elif j == 3:
+            wait("V", ("t6", 1))
+            inc(V.tensor_scalar(ti(7), m, 11, 2, ALU.arith_shift_right, ALU.bitwise_and), "t7")
+            inc(V.tensor_scalar(ti(8), m, -8192, None, ALU.bitwise_and), "t11")
+        elif j == 4:
+            wait("V", ("t7", 1), ("t3", 1))
+            inc(V.tensor_tensor(ti(10), ti(3), ti(7), ALU.max), "t8")
+            inc(V.tensor_scalar(ti(9), m, P - 1, None, ALU.bitwise_and), "t11")
+        elif j == 5:
+            wait("V", ("t8", 1))
+            inc(V.tensor_scalar(ti(11), ti(10), float(rank), None, ALU.add), "t9")
+        elif j == 6:
+            wait("V", ("t9", 1))
+            inc(V.tensor_scalar(ti(12), ti(11), nr - 1, None, ALU.bitwise_and), "t10")
+        else:
+            wait("V", ("t10", 1))
+            inc(V.tensor_scalar(T.tf[:, 0, :], ti(12), -last, None, ALU.add), "t11")
+
+    def results(n, j):
+        s, a, b, w = span(n)
+        ft = lambda role: (role + "_" + str(n % NH), FIN[role])
+        m, thr, new, keep = T.mo[:, 4, a:b], T.ti[:, 8, a:b], T.ti[:, 13, a:b], T.tf[:, 1, a:b]
+        if j == 0:
+            wait("V", ("t11", 3), tok("m4", n))
+            rinc(V.tensor_tensor(new, m, thr, ALU.min), "fn", n)
+            rinc(V.tensor_tensor(keep, m, thr, ALU.is_ge), "fk", n)
+        elif j == 1:
+            wait("V", ft("fn"))
+            rinc(V.tensor_scalar(T.ti[:, 14, a:b], new, 13, None, ALU.arith_shift_right), "fc", n)
+            rinc(V.tensor_scalar(T.ti[:, 15, a:b], new, P - 1, None, ALU.bitwise_and), "fp", n)
+            wait("V", ft("fk"))
+            rinc(V.tensor_tensor(T.tf[:, 3, a:b], keep, T.tf[:, 0, a:b], ALU.mult), "ff", n)
+            rinc(V.tensor_tensor(T.tf[:, 2, a:b], keep, T.ti[:, 9, a:b], ALU.mult), "fp", n)
+        elif j == 2:
+            wait("V", ft("fc"))
+            rinc(V.tensor_scalar(T.oc[:, a:b], T.ti[:, 14, a:b], float(MID), None, ALU.add), "yc", n)
+            if n == NN - 1:
+                wait("S", ft("ff"))
+                rinc(S.activation(T.of[:, a:b], T.tf[:, 3, a:b], ACT.Identity, bias=last), "yf", n)
+            else:
+                wait("V", ft("ff"))
+                rinc(V.tensor_scalar(T.of[:, a:b], T.tf[:, 3, a:b], last, None, ALU.add), "yf", n)
+            wait("V", ft("fp"))
+            rinc(V.tensor_tensor(T.op[:, a:b], T.tf[:, 2, a:b], T.ti[:, 15, a:b], ALU.add), "yp", n)
+
+    def emit(e, stage, n):
+        s, a, b, w = span(n)
+        q = 16 * w
+        u = T.ua[:, int(s == GUEST), 16 * a:16 * b]
+        ke, kl = ps("pc", n)[:, KE:KE + 2 * w], ps("pl", n)[:, 0:2 * w]
+        if stage[0] in "gsab" and stage[1:].isdigit():
+            c = int(stage[1])
+            k, route = POS[c], ROUTES[s][c]
+            gd, sq = T.gd[:, n, k * q:(k + 1) * q], T.sq[:, n, k * q:(k + 1) * q]
+            pb = T[bank(c, n)][:, 0:q]
+        if stage == "xy":
+            wait("V", there(n))
+            rinc(V.tensor_scalar(T.xyi[:, s, 0, a:b], k_in(s, a, b), 63, None, ALU.bitwise_and), "xy", n)
+            rinc(V.tensor_scalar(T.xyi[:, s, 1, a:b], k_in(s, a, b), 6, 63, ALU.arith_shift_right, ALU.bitwise_and), "xy", n)
+        elif stage == "cv":
+            wait("V", tok("xy", n), ("c1", 4))
+            src = T.xyi[:, s, :, a:b]
+            rinc(V.tensor_copy(T.xyb[:, 4 * s:4 * s + 2, 2 + a:2 + b], src), "cv", n)
+            rinc(V.tensor_scalar(T.xyb[:, 4 * s + 2:4 * s + 4, 2 + a:2 + b], src, 1.0, 63.0, ALU.add, ALU.min), "cv", n)
+        elif stage == "cc":
+            wait("PE", tok("cv", n), tok("cv", n - 1), tok("kc", n - 2), *j_tok[s])
+            pl = lambda k, d: T.xyb[:, 4 * s + k, 2 + a - d:2 + b - d]
+            jp = lambda k: T.fa[:, SLOT[s], k * K + a:k * K + b]
+            e1, e64 = T.eye[:], T.eye64[:]
+            groups = [[(e64, pl(1, 0)), (e1, pl(0, 0))],
+                      [(e64, pl(3, 2)), (e1, pl(0, 2))],
+                      [(T.sh[:, 1, :], pl(1, 0)), (T.sh[:, 0, :], pl(2, 0)), (T.wr[:, 1, :], pl(1, 1)), (T.wr[:, 0, :], pl(2, 1))],
+                      [(e64, pl(1, 0)), (e1, pl(0, 0)), (e64, jp(0)), (e1, jp(1))]]
+            for k, grp in enumerate(groups):
+                for j, (l, r) in enumerate(grp):
+                    ins = PE.matmul(ps("pc", n)[:, k * w:(k + 1) * w], l, r, j == 0, j == len(grp) - 1)
+                rinc(ins, "cc", n)
+        elif stage == "off":
+            wait("V", tok("cc", n))
+            rinc(V.tensor_scalar(T.off[:, n, 0:4 * w], ps("pc", n)[:, 0:4 * w], 0.0, float(P - 1), ALU.max, ALU.min), "off", n)
+        elif stage == "plc":
+            wait("V", tok("off", n))
+            rinc(V.tensor_scalar(T.plc[:, n, 0:4 * w], T.off[:, n, 0:4 * w], -2048.0, None, ALU.add), "plc", n)
+        elif stage[0] == "g":
+            win = T.fa[:, SLOT[s], J:J + P].indirect(T.off[:, n, k * w:(k + 1) * w])
+            wait(e, tok("off", n), *f_tok[s])
+            if route == "V":
+                wait(e, u_tok(s))
+                rinc(V.tensor_tensor(gd, win, u, ALU.subtract), stage, n)
+            else:
+                rinc(S.activation(gd, win, ACT.Copy), stage, n)
+        elif stage[0] == "a":
+            before = [tok("s%d" % x, m) for m in range(n) for x in through(m) if bank(x, m) == bank(c, n)]
+            wait("PE", u_tok(s), *before[-1:])
+            PE.matmul(pb, T.eyem[:, int(route == "M"), :], u, True, False)
+        elif stage[0] == "b":
+            wait("PE", tok("g%d" % c, n))
+            rinc(PE.matmul(pb, T.eye[:], gd, False, True), stage, n)
+        elif stage[0] == "s":
+            wait(e, tok("g%d" % c, n) if route == "V" else formed(c, n))
+            if route == "M":
+                rinc(V.tensor_tensor(sq, pb, gd, ALU.mult), stage, n)
+            else:
+                rinc(S.activation(sq, gd if route == "V" else pb, ACT.Square), stage, n)
+        elif stage == "pre":
+            wait("PE", tok("plc", n), tok("m1", n - 2), n_tok(s))
+            for j, kk in enumerate((ke, kl)):
+                table = ROUTES[s][2 + j] == "M"
+                PE.matmul(kk, T.eyeh[:], T.plc[:, n, 2 * j * w:2 * (j + 1) * w], True, False)
+                PE.matmul(kk, T.cl[0:65, :], T.ct[0:65, n % NH + (0 if table else NH), j, 0:2 * w], False, False)
+                if table:
+                    PE.matmul(kk, T.eyek[:], T.nq[:, int(s == GUEST), 2 * a:2 * b], False, False)
+        elif stage in ("ke", "kl"):
+            j = int(stage == "kl")
+            wait("PE", tok("s%d" % j, n), tok("s%d" % (2 + j), n))
+            for r in range(16):
+                ins = PE.matmul((ke, kl)[j], T.sel[:, 15 - r:143 - r], T.sq[:, n, 2 * j * q + r:2 * (j + 1) * q:16], False, r == 15)
+            rinc(ins, stage, n)
+        elif stage == "kc":
+            wait("S", tok("ke", n))
+            rinc(S.activation(T.kec[:, n, 0:2 * w], ke, ACT.Copy), "kc", n)
+        elif stage == "m1":
+            wait("V", tok("kc", n), tok("kl", n))
+            rinc(V.tensor_tensor(T.ab[:, n, 0:2 * w], kl, T.kec[:, n, 0:2 * w], ALU.min), "m1", n)
+        elif stage == "m2":
+            wait("V", tok("m1", n))
+            rinc(V.tensor_scalar(T.abc[:, n, 0:2 * w], T.ab[:, n, 0:2 * w], -4097, None, ALU.bitwise_and), "m2", n)
+        elif stage == "m3":
+            wait("V", tok("m2", n))
+            rinc(V.tensor_scalar(T.bs[:, n, 0:w], T.abc[:, n, w:2 * w], 4096.0, None, ALU.add), "m3", n)
+        elif stage == "m4":
+            wait("V", tok("m3", n))
+            rinc(V.tensor_tensor(k_out(s, a, b), T.abc[:, n, 0:w], T.bs[:, n, 0:w], ALU.min), "m4", n)
+        elif stage[0] == "q" and n in BEST_AT:
+            best(BEST_AT[n], int(stage[1]))
+        elif stage[0] == "q" and n > NN - NH:
+            results(n - 1, int(stage[1]))
+
+    for n in range(NH):
+        emit("V", "xy", n)
+    wait("V", ("ldj", 16))
+    inc(V.tensor_scalar(T.jint[:, 0:K], T.jraw[:], 6, None, ALU.arith_shift_right), "j0")
+    inc(V.tensor_scalar(T.jint[:, K:2 * K], T.jraw[:], 63, None, ALU.bitwise_and), "j0")
+    for n in range(NH):
+        emit("V", "cv", n)
+    wait("V", ("j0", 2))
+    inc(V.tensor_copy(T.fa[:, 0, 0:J], T.jint[:]), "j1")
     wait("S", ("ldu", 16))
     inc(S.activation(T.usq[:], T.ua[:, 0, :], ACT.Square), "us")
-    wait("PE", ("us", 1), ("c7", 5), ("c1", 4))
+    wait("PE", ("us", 1))
+    for r in range(16):
+        ins = PE.matmul(T.pl1[:, 0:K], T.sel[:, 15 - r:143 - r], T.usq[:, r:Q:16], r == 0, r == 15)
+    inc(ins, "nu")
+    wait("V", ("nu", 1))
+    for h in range(NH):
+        s, a, b, w = span(h)
+        inc(V.tensor_scalar(T.nq[:, 0, 2 * a + w:2 * b], T.pl1[:, a:b], 1.0 / 8192, -float(MID), ALU.mult, ALU.add), "nk")
+    for n in range(NH):
+        emit("PE", "cc", n)
+        emit("V", "off", n)
+    for n in range(NH):
+        emit("V", "plc", n)
 
-    def t_norms():
-        for r in range(16):
-            ins = PE.matmul(T.pkl1[:, 0:K], T.sel[:, 15 - r:143 - r], T.usq[:, r:Q:16], r == 0, r == 15)
-        inc(ins, "nu")
+    done = [(stage, n) for stage in ("xy", "cv", "cc", "off", "plc") for n in range(NH)]
+    for e in ("V", "S", "PE"):
+        for i in range(NN + 1):
+            for stage, d in (AWAY if i < (GUEST + 1) * NH else HOME)[e]:
+                if 0 <= i + d < NN and (stage, i + d) not in done:
+                    done.append((stage, i + d))
+                    emit(e, stage, i + d)
+    for j in range(3):
+        results(NN - 1, j)
 
-    def table():
-        wait("V", ("nu", 1))
-        for h in range(2):
-            for c in (W, 3 * W):
-                a = 2 if (h == 0 and c == W) else 0
-                inc(V.tensor_scalar(T.nk[:, 0, h * 4 * W + c + a:h * 4 * W + c + W], T.pkl1[:, h * W + a:(h + 1) * W],
-                                    1.0 / 8192, -float(MID), ALU.mult, ALU.add), "nk1")
+    sent = 0
+    wait("G", ("nk", NH), ("c10", 3))
+    sent += write(g, T, topo, peer(1), T.nq[:, 1, :], T.nq[:, 0, :], "an", topo.engines(core, peer(1)))
+    wait("G", ("ldu", 16), *own_f)
+    sent += write(g, T, topo, peer(1), T.ua[:, 1, :], T.ua[:, 0, :], "au", topo.engines(core, peer(1)))
+    for k, (a, b, h) in enumerate(FEEDS):
+        wait("G", *loaded(a, b))
+        part = T.fa[:, 0, J + a:J + b]
+        sent += write(g, T, topo, helpers_of(T, topo, rank)[h], part, part, "hp%d" % k, near_engines(T, topo, rank))
+    for n in range((GUEST + 1) * NH):
+        s, a, b, w = span(n)
+        dst = peer(-1 if s == GUEST else 1)
+        wait("G", tok("m4", n))
+        sent += write(g, T, topo, dst, k_in(s + 1, a, b), k_out(s, a, b), "arr%d" % (n + NH), topo.engines(core, dst))
+        for x in OWN.get(n, ()):
+            sent += hand_on(g, core, T, topo, rank, *x)
+    total["sent"] = sent
 
-    NKT = [("nk2", 3), ("nk1", 4)]
-    NN = NE // max(len(UD), 1)
-    u_tok = [("au%d" % d, NE) if d else ("ldu", 16) for d in LOC]
-    n_tok = [[("an%d" % d, NN)] if d else NKT for d in LOC]
-    f_tok = [("afb%d" % FD.index(d), NP * NE) if d else ("ldf", 16) for d in FO]
-    j_tok = [("afb%d" % FD.index(d), NP * NE) if d else ("j1", 1) for d in FO]
-    frame = lambda s, a, b: T.fb[:, FD.index(FO[s]), a:b] if FO[s] else T.fa[:, a:b]
-    hop = lambda s: (LOC[s] - LOC[s - 1]) % n
-
-    def state(s, h, a, b):
-        if s == 0:
-            return T.mi[:, 0, a:b], ("lds", 16)
-        if hop(s):
-            return T.mi[:, s, a:b], ("arr%d_%d" % (s, h), NE)
-        return T.mo[:, s - 1, a:b], tok("mm", s - 1, h)
-
-    def result(s):
-        if LOC[s] == 0:
-            return T.mo[:, s, :], [tok("mm", s, 0), tok("mm", s, 1)]
-        if LOC[s + 1] == 0:
-            return T.mi[:, s + 1, :], [("arr%d_%d" % (s + 1, h), NE) for h in range(2)]
-        return T.mh[:, s, :], [("amh%d" % s, NE)]
-
-    def v_split(s, h, a, b, between=None):
-        m, t = state(s, h, a, b)
-        wait("V", t)
-        rinc(V.tensor_scalar(T.xyi[:, s, 0, a:b], m, 63, None, ALU.bitwise_and), "xy", h)
-        rinc(V.tensor_scalar(T.xyi[:, s, 1, a:b], m, 6, 63, ALU.arith_shift_right, ALU.bitwise_and), "xy", h)
-        if between:
-            between()
-        wait("V", tok("xy", s, h))
-        src = T.xyi[:, s, :, a:b]
-        rinc(V.tensor_copy(T.xyb[:, 4 * s:4 * s + 2, 2 + a:2 + b], src), "cv", h)
-        rinc(V.tensor_scalar(T.xyb[:, 4 * s + 2:4 * s + 4, 2 + a:2 + b], src, 1.0, 63.0, ALU.add, ALU.min), "cv", h)
-
-    def v_jumps():
-        wait("V", ("ldj", 16))
-        inc(V.tensor_scalar(T.jint[:, 0:K], T.jraw[:], 6, None, ALU.arith_shift_right), "j0")
-        inc(V.tensor_scalar(T.jint[:, K:2 * K], T.jraw[:], 63, None, ALU.bitwise_and), "j0")
-
-    def v_off(s, h):
-        i = 2 * s + h
-        wait("V", tok("cc", s, h))
-        rinc(V.tensor_scalar(T.off[:, i, :], T["pck%d" % h][:, 0:4 * W], 0.0, float(P - 1), ALU.max, ALU.min), "off", h)
-
-    def v_plc(s, h):
-        i = 2 * s + h
-        wait("V", tok("off", s, h))
-        rinc(V.tensor_scalar(T.plc[:, i, :], T.off[:, i, :], -2048.0, None, ALU.add), "plc", h)
-
-    def v_main(s, h):
-        i = 2 * s + h
-        u = T.ua[:, LOC[s], 512 * h:512 * (h + 1)]
-        win = frame(s, 0, P)
-        wait("V", tok("off", s, h), f_tok[s], u_tok[s])
-        rinc(V.tensor_tensor(T.dd[:, i, 0:512], win.indirect(T.off[:, i, 0:W]), u, ALU.subtract), "g0", h)
-        rinc(V.tensor_tensor(T.dd[:, i, 512:Q], win.indirect(T.off[:, i, 2 * W:3 * W]), u, ALU.subtract), "g1", h)
-        wait("V", tok("b2", s, h))
-        rinc(V.tensor_tensor(T.sqe[:, i, 512:Q], T["pb2%d" % h][:], T.gg[:, i, 0:512], ALU.mult), "m2", h)
-        wait("V", tok("b3", s, h))
-        rinc(V.tensor_tensor(T.sql[:, i, 512:Q], T["pb3%d" % h][:], T.gg[:, i, 512:Q], ALU.mult), "m3", h)
-
-    def v_min(s, h):
-        i = 2 * s + h
-        wait("V", tok("kc", s, h), tok("kl", s, h))
-        rinc(V.tensor_tensor(T.ab[:, i, :], T["pkl%d" % h][:, 0:K], T.kec[:, i, :], ALU.min), "ab", h)
-        wait("V", tok("ab", s, h))
-        rinc(V.tensor_scalar(T.abc[:, i, :], T.ab[:, i, :], -4097, None, ALU.bitwise_and), "ac", h)
-        wait("V", tok("ac", s, h))
-        rinc(V.tensor_scalar(T.bs[:, i, :], T.abc[:, i, W:K], 4096.0, None, ALU.add), "bs", h)
-        wait("V", tok("bs", s, h))
-        rinc(V.tensor_tensor(T.mo[:, s, h * W:(h + 1) * W], T.abc[:, i, 0:W], T.bs[:, i, :], ALU.min), "mm", h)
-
-    fr = [float((rank + s) % n) for s in range(4)]
-    ti = lambda k: T.ti[:, k, :]
-    tf = lambda k: T.tf[:, k, :]
-
-    def best_a():
-        m, t = result(0)
-        wait("V", *t)
-        inc(V.tensor_scalar(ti(0), m, -8192, None, ALU.bitwise_and), "t0")
-        inc(V.tensor_scalar(ti(1), m, P - 1, None, ALU.bitwise_and), "t0")
-
-    def best_b():
-        m, t = result(1)
-        wait("V", ("t0", 2), *t)
-        inc(V.tensor_tensor(tf(0), m, ti(0), ALU.is_ge), "t1")
-        inc(V.tensor_tensor(ti(2), m, ti(0), ALU.min), "t1")
-        wait("V", ("t1", 2))
-        inc(V.tensor_scalar(ti(3), ti(2), -8192, None, ALU.bitwise_and), "t2")
-        inc(V.tensor_scalar(ti(4), ti(2), P - 1, None, ALU.bitwise_and), "t2")
-        inc(V.tensor_tensor(tf(1), tf(0), ti(1), ALU.mult), "t2")
-        inc(V.tensor_scalar(tf(2), tf(0), fr[0] - fr[1], fr[1] - fr[2], ALU.mult, ALU.add), "t2")
-        wait("V", ("t2", 4))
-        inc(V.tensor_tensor(tf(3), tf(1), ti(4), ALU.add), "t3")
-
-    def best_c():
-        m, t = result(2)
-        wait("V", ("t3", 1), *t)
-        inc(V.tensor_tensor(tf(4), m, ti(3), ALU.is_ge), "t4")
-        inc(V.tensor_tensor(ti(5), m, ti(3), ALU.min), "t4")
-        wait("V", ("t4", 2))
-        inc(V.tensor_scalar(ti(6), ti(5), -8192, None, ALU.bitwise_and), "t5")
-        inc(V.tensor_scalar(ti(7), ti(5), P - 1, None, ALU.bitwise_and), "t5")
-        inc(V.tensor_tensor(tf(5), tf(4), tf(3), ALU.mult), "t5")
-        inc(V.tensor_tensor(tf(6), tf(4), tf(2), ALU.mult), "t5")
-        wait("V", ("t5", 4))
-        inc(V.tensor_tensor(tf(7), tf(5), ti(7), ALU.add), "t6")
-        inc(V.tensor_scalar(tf(8), tf(6), fr[2] - fr[3], None, ALU.add), "t6")
-
-    def best_d():
-        m, t = result(3)
-        wait("V", ("t6", 2), *t)
-        inc(V.tensor_tensor(ti(8), m, ti(6), ALU.min), "t7")
-        inc(V.tensor_tensor(tf(9), m, ti(6), ALU.is_ge), "t8")
-        wait("V", ("t7", 1))
-        inc(V.tensor_scalar(ti(9), ti(8), 13, None, ALU.arith_shift_right), "t9")
-        inc(V.tensor_scalar(ti(10), ti(8), P - 1, None, ALU.bitwise_and), "t10")
-        wait("V", ("t8", 1))
-        inc(V.tensor_tensor(tf(10), tf(9), tf(7), ALU.mult), "t10")
-        inc(V.tensor_tensor(tf(11), tf(9), tf(8), ALU.mult), "t11")
-        wait("V", ("t9", 1))
-        inc(V.tensor_scalar(T.oc[:], ti(9), float(MID), None, ALU.add), "t12")
-        wait("V", ("t10", 2))
-        inc(V.tensor_tensor(T.op[:], tf(10), ti(10), ALU.add), "t13")
-        wait("S", ("t11", 1))
-        inc(S.activation(T.of[:], tf(11), ACT.Identity, bias=fr[3]), "t11")
-
-    v_split(0, 0, 0, K, v_jumps)
-    wait("V", ("j0", 2))
-    inc(V.tensor_copy(T.fa[:, P:FW], T.jint[:]), "j1")
-    v_off(0, 0)
-    v_off(0, 1)
-    v_plc(0, 0)
-    v_plc(0, 1)
-    table()
-    for s in range(4):
-        for h in range(2):
-            if s > 0:
-                v_off(s, h)
-                v_plc(s, h)
-            v_main(s, h)
-            ns, nh = (s, 1) if h == 0 else (s + 1, 0)
-            if (s, h) == (1, 0):
-                best_a()
-            if (s, h) == (2, 1):
-                best_b()
-            if (s, h) == (3, 1):
-                best_c()
-            if 0 < ns < 4:
-                v_split(ns, nh, nh * W, (nh + 1) * W)
-            v_min(s, h)
-
-    for s in range(4):
-        for h in range(2):
-            i = 2 * s + h
-            win = frame(s, 0, P)
-            wait("S", tok("off", s, h), f_tok[s])
-            rinc(S.activation(T.gg[:, i, 0:512], win.indirect(T.off[:, i, W:2 * W]), ACT.Copy), "g2", h)
-            rinc(S.activation(T.gg[:, i, 512:Q], win.indirect(T.off[:, i, 3 * W:4 * W]), ACT.Copy), "g3", h)
-            wait("S", tok("g0", s, h))
-            rinc(S.activation(T.sqe[:, i, 0:512], T.dd[:, i, 0:512], ACT.Square), "s0", h)
-            wait("S", tok("g1", s, h))
-            rinc(S.activation(T.sql[:, i, 0:512], T.dd[:, i, 512:Q], ACT.Square), "s1", h)
-            wait("S", tok("ke", s, h))
-            rinc(S.activation(T.kec[:, i, :], T["pck%d" % h][:, 128:128 + K], ACT.Copy), "kc", h)
-    best_d()
-
-    def t_cand(s, h):
-        wait("PE", tok("cv", s, h), ("c5", 4), ("c6", 2), ("c2", 1), j_tok[s])
-        if h == 1:
-            wait("PE", tok("cv", s, 0))
-        pl = lambda k, d: T.xyb[:, 4 * s + k, 2 + h * W - d:2 + (h + 1) * W - d]
-        jp = lambda k: frame(s, P + k * K + h * W, P + k * K + (h + 1) * W)
-        e1, e64 = T.eye[:], T.eye64[:]
-        groups = [[(e64, pl(1, 0)), (e1, pl(0, 0))],
-                  [(e64, pl(3, 2)), (e1, pl(0, 2))],
-                  [(T.sh[:, 1, :], pl(1, 0)), (T.sh[:, 0, :], pl(2, 0)), (T.wr[:, 1, :], pl(1, 1)), (T.wr[:, 0, :], pl(2, 1))],
-                  [(e64, pl(1, 0)), (e1, pl(0, 0)), (e64, jp(0)), (e1, jp(1))]]
-        for k, grp in enumerate(groups):
-            for j, (a, b) in enumerate(grp):
-                ins = PE.matmul(T["pck%d" % h][:, k * W:(k + 1) * W], a, b, j == 0, j == len(grp) - 1)
-            rinc(ins, "cc", h)
-
-    def t_main(s, h):
-        i = 2 * s + h
-        u = T.ua[:, LOC[s], 512 * h:512 * (h + 1)]
-        ke, kl = T["pck%d" % h][:, 128:128 + K], T["pkl%d" % h][:, 0:K]
-        b2, b3 = T["pb2%d" % h][:], T["pb3%d" % h][:]
-        wait("PE", u_tok[s])
-        PE.matmul(b2, T.eyem2[:], u, True, False)
-        PE.matmul(b3, T.eyem2[:], u, True, False)
-        wait("PE", tok("g2", s, h))
-        rinc(PE.matmul(b2, T.eye[:], T.gg[:, i, 0:512], False, True), "b2", h)
-        wait("PE", tok("plc", s, h), *n_tok[s])
-        for j, kk in enumerate((ke, kl)):
-            PE.matmul(kk, T.eyeh[:], T.plc[:, i, j * K:(j + 1) * K], True, False)
-            PE.matmul(kk, T.eyek[:], T.nk[:, LOC[s], h * 4 * W + j * K:h * 4 * W + (j + 1) * K], False, False)
-            PE.matmul(kk, T.eyeh[:], T.low[:, j * K:(j + 1) * K], False, False)
-        wait("PE", tok("g3", s, h))
-        rinc(PE.matmul(b3, T.eye[:], T.gg[:, i, 512:Q], False, True), "b3", h)
-        for kk, sq, a, b, role in ((ke, T.sqe, "s0", "m2", "ke"), (kl, T.sql, "s1", "m3", "kl")):
-            wait("PE", tok(a, s, h), tok(b, s, h))
-            for r in range(16):
-                ins = PE.matmul(kk, T.sel[:, 15 - r:143 - r], sq[:, i, r:Q:16], False, r == 15)
-            rinc(ins, role, h)
-
-    t_norms()
-    t_cand(0, 0)
-    t_cand(0, 1)
-    for s in range(4):
-        for h in range(2):
-            t_main(s, h)
-            ns, nh = (s, 1) if h == 0 else (s + 1, 0)
-            if 0 < ns < 4:
-                t_cand(ns, nh)
-
-    wait("G", ("ldu", 16))
-    for d in UD:
-        send(peer(d), T.ua[:, d, :], T.ua[:, 0, :], "au%d" % d)
-    if UD:
-        wait("G", *NKT)
-        trs = []
-        for j, d in enumerate(UD):
-            rid, pid, _ = topo.addr(peer(d))
-            engs = topo.engines(core, peer(d))[j * NN:(j + 1) * NN]
-            trs.append(RemoteDMATransfer(dst_ids=[DstId(rid=rid, pnc=pid)], dma_engine_mask=mask_of(engs),
-                                         remote_sem=T.sem["an%d" % d], src=T.nk[:, 0, :], dst=T.nk[:, d, :]))
-        g.remote_dma_fused(trs, local_sem=T.sem.sent)
-        total["sent"] += NN * len(UD)
-    hp = helpers_of(T, topo, rank)[0]
-    near = near_engines(topo, core, hp, peer(1))
-    w = FW // NP
-
-    def piece(k):
-        wait("G", ("ldf", 16))
-        if k == NP - 1:
-            wait("G", ("j1", 1))
-        send(hp, T.fb[:, 0, k * w:(k + 1) * w], T.fa[:, k * w:(k + 1) * w], "hp%d" % k, near)
-
-    early = NP // 2 if FO[1] == 0 and FO[2] == 0 else NP
-    for k in range(early):
-        piece(k)
-    for s in range(3):
-        for h in range(2):
-            if hop(s + 1):
-                wait("G", tok("mm", s, h))
-                send(peer(hop(s + 1)), T.mi[:, s + 1, h * W:(h + 1) * W], T.mo[:, s, h * W:(h + 1) * W], "arr%d_%d" % (s + 1, h))
-            if (s, h) == (0, 0):
-                for k in range(early, NP):
-                    piece(k)
-        if LOC[s] and LOC[s + 1]:
-            wait("G", tok("mm", s, 0), tok("mm", s, 1))
-            send(peer(-LOC[s]), T.mh[:, s, :], T.mo[:, s, :], "amh%d" % s)
-
-    wait("SY", ("t12", 1))
-    inc(SY.dma_start(T.yc[:], T.oc[:]), "sty", 16)
-    wait("S", ("t11", 2))
-    inc(S.dma_start(T.yf[:], T.of[:]), "sty", 16)
-    wait("SY", ("t13", 1))
-    inc(SY.dma_start(T.yp[:], T.op[:]), "sty", 16)
+    for q, out, src in (("SY", "yc", T.oc), ("S", "yf", T.of), ("SY", "yp", T.op)):
+        wait(q, *[(out + "_" + str(h), 1) for h in range(NH)])
+        inc(Qs[q].dma_start(T[out][:], src[:]), "sty", 16)
     waited = {}
     for q in seen:
         for k, v in seen[q].items():

@@ -12,23 +12,24 @@ MID, BIG = 1800, 4096.0
 HALF = "float16"
 GUEST = 1
 SLOT = (0, 0, 1, 2)
-ROUTES = ("VVMM", "VVMM", "VSVM", "VSVM")
+ROUTES = ["VVMM"] * 4 + ["VVMS"] * 3 + ["VVMM"]
 POS = (0, 2, 1, 3)
 
 LOADS = ("u", (0, P))
-FEEDS = ((1664, 2272, 0), (2272, 2880, 1), (2880, 3488, 0), (3488, P, 1))
-HELP = [[(a, b, s) for s in (2, 3) for a, b, x in FEEDS if x == h] for h in range(2)]
-OWN = {0: ((-J, 768, 2),), 1: ((768, 1664, 2),), 2: ((-J, 768, 3),), 3: ((768, 1664, 3),)}
+OWN = ((-J, 512, 2), (512, 1536, 2), (-J, 896, 3), (896, 2176, 3))
+FEEDS = ((2176, 2816, 1), (1536, 2176, 0), (2816, 3456, 1), (3456, P, 0))
+HELP = [[(a, b, s) for s in (2, 3) for a, b, x in FEEDS if x == h and (s == 2 or a >= OWN[3][1])] for h in range(2)]
 
-AWAY = {"V": [("g0", 0), ("plc", 0), ("g1", 0), ("s2", 0), ("s3", 0), ("xy", 1), ("cv", 1),
-              ("m1", 0), ("m2", 0), ("m3", 0), ("m4", 0), ("off", 1)],
-        "S": [("g2", 0), ("g3", 0), ("s0", 0), ("s1", 0), ("kc", 0)],
-        "PE": [("a2", 0), ("a3", 0), ("pre", 0), ("b2", 0), ("b3", 0), ("ke", 0), ("kl", 0), ("cc", 1)]}
-HOME = {"V": [("g0", 0), ("m1", -1), ("q2", -1), ("m2", -1), ("g2", 0), ("m3", -1), ("q3", -1), ("plc", 0), ("q4", -1),
-              ("q5", -1), ("m4", -1), ("xy", 1), ("q6", -1), ("cv", 1), ("s3", 0), ("q7", -1), ("q0", 0), ("off", 1), ("q1", 0)],
-        "S": [("g1", 0), ("g3", 0), ("s0", 0), ("s2", 0), ("s1", 0), ("kc", 0)],
-        "PE": [("a1", 0), ("b1", 0), ("a3", 0), ("b3", 0), ("pre", 0), ("cc", 1), ("ke", 0), ("kl", 0)]}
-BEST_AT = {2 * NH: 1, 3 * NH: 2}
+AWAY = {"V": [("g0", 0), ("g1", 0), ("s2", 0), ("s3", 0), ("xy", 1), ("cv", 1),
+              ("m1", 0), ("m2", 0), ("off", 1), ("of2", 1), ("m3", 0), ("plc", 1), ("m4", 0)],
+        "S": [("g2", 0), ("g3", 0), ("s0", 0), ("s1", 0), ("t", 0), ("kc", 0)],
+        "PE": [("a2", 0), ("a3", 0), ("b2", 0), ("pre", 0), ("b3", 0), ("a2", 1), ("ke", 0), ("kl", 0), ("km", 0),
+               ("cc", 1), ("cd", 1), ("a3", 1)]}
+FIRST = dict(AWAY, V=AWAY["V"][:4] + [("g0", 1)] + AWAY["V"][4:])
+HOME = {"V": [("g0", 0), ("m1", -1), ("plc", 0), ("q2", -1), ("m2", -1), ("g1", 0), ("m3", -1), ("s2", 0), ("m4", -1),
+              ("u2", 0), ("s3", 0), ("xy", 1), ("q0", 0), ("cv", 1), ("q1", 0), ("off", 1), ("of2", 1)],
+        "S": [("g2", 0), ("g3", 0), ("s0", 0), ("s1", 0), ("s3", 0), ("t", 0), ("kc", 0)],
+        "PE": [("b2", 0), ("a3", 1), ("b3", 0), ("pre", 0), ("a2", 1), ("ke", 0), ("cc", 1), ("cd", 1), ("kl", 0), ("km", 0)]}
 
 SCRATCH = {
     "fa": ("sbuf", [128, 3, J + P], "bfloat16"),
@@ -47,7 +48,7 @@ SCRATCH = {
     "cl": ("sbuf", [128, 128], "bfloat16"), "ct": ("sbuf", [128, 2 * NH, 2, 2 * W], "bfloat16"),
     "blk": ("sbuf", [128, 16], "bfloat16"), "sel": ("sbuf", [128, 144], "bfloat16"),
     "pen": ("sbuf", [128, 16], "float32"),
-    "ti": ("sbuf", [128, 16, K], "int32"), "tf": ("sbuf", [128, 4, K], "float32"),
+    "ti": ("sbuf", [128, 16, K], "int32"), "tf": ("sbuf", [128, 8, K], "float32"),
     "oc": ("sbuf", [128, K], "float32"), "of": ("sbuf", [128, K], "float32"), "op": ("sbuf", [128, K], "float32"),
 }
 for _h in range(2):
@@ -55,14 +56,15 @@ for _h in range(2):
         SCRATCH[_n + str(_h)] = ("psum", [128, 512], "float32")
 KE = 256
 
-ROLES = {"xy": 2, "cv": 2, "cc": 4, "off": 1, "plc": 1, "g0": 1, "g1": 1, "g2": 1, "g3": 1, "s0": 1, "s1": 1, "s2": 1, "s3": 1,
-         "b1": 1, "b2": 1, "b3": 1, "ke": 1, "kl": 1, "kc": 1, "m1": 1, "m2": 1, "m3": 1, "m4": 1}
+ROLES = {"xy": 2, "cv": 2, "cc": 1, "cd": 1, "off": 1, "of2": 1, "plc": 1, "g0": 1, "g1": 1, "g2": 1, "g3": 1,
+         "s0": 1, "s1": 1, "s2": 1, "s3": 1, "t": 1, "u2": 1, "b2": 1, "b3": 1, "ke": 1, "km": 1, "kc": 1,
+         "m1": 1, "m2": 1, "m3": 1, "m4": 1}
 FIN = {"fn": 1, "fk": 1, "fc": 1, "fp": 2, "ff": 1, "yc": 1, "yp": 1, "yf": 1}
 SEMAPHORES = ([r + "_" + str(h) for r in list(ROLES) + list(FIN) for h in range(NH)]
               + ["ldf%d" % k for k in range(len(LOADS))] + ["hp%d" % k for k in range(len(FEEDS))]
               + ["arr%d" % n for n in range(NH, 3 * NH)] + [a + str(k) for a in ("af", "aj") for k in (2, 3)]
               + [a + str(k) for a in "tc" for k in range(12)]
-              + ["ldu", "lds", "ldj", "sty", "sent", "j0", "j1", "us", "nu", "nk", "au", "an"])
+              + ["ldu", "lds", "ldj", "sty", "sent", "j0", "j1", "us", "nu", "nk", "an", "ag"] + ["au%d" % h for h in range(NH)])
 
 
 def mask_of(engs):
@@ -89,10 +91,13 @@ def write(g, T, topo, dst, out, in_, sem, engs):
     return len(engs)
 
 
-def hand_on(g, core, T, topo, rank, a, b, s):
+def hand_on(g, core, T, topo, rank, a, b, s, slot=0):
     dst = T.cores[rank - s]
-    return write(g, T, topo, dst, T.fa[:, SLOT[s], J + a:J + b], T.fa[:, 0, J + a:J + b], ("aj%d" if a < 0 else "af%d") % s,
-                 topo.engines(core, dst))
+    return write(g, T, topo, dst, T.fa[:, SLOT[s], J + a:J + b], T.fa[:, slot, J + a:J + b], landed(a, b, s), topo.engines(core, dst))
+
+
+def landed(a, b, s):
+    return "aj%d" % s if a < 0 else "ag" if (a, b, s) == OWN[1] else "af%d" % s
 
 
 def helper_program(g, core, T, topo, rank, h):
@@ -130,8 +135,11 @@ def rank_program(g, core, T, topo):
         ins.then_inc(T.sem[name], k)
         total[name] = total.get(name, 0) + k
 
+    home = lambda n: n >= (GUEST + 1) * NH
+    halved = lambda n: 3 if ROUTES[n][3] == "S" else 1
+
     def tok(role, n):
-        return (role + "_" + str(n % NH), (n // NH + 1) * ROLES[role] if n >= 0 else 0)
+        return (role + "_" + str(n % NH), ROLES[role] * len([m for m in range(n % NH, n + 1, NH) if role != "u2" or home(m)]))
 
     def rinc(ins, role, n):
         inc(ins, role + "_" + str(n % NH))
@@ -191,20 +199,16 @@ def rank_program(g, core, T, topo):
     inc(V.tensor_scalar(T.sh[:, 1, 1:128], T.eye[:, 0:127], T.pen[:, 8:9], 64.0, ALU.mult, ALU.mult), "c5")
     wait("PE", ("c7", total["c7"]), ("c1", 4), ("c5", 4), ("c6", 3), ("c2", 1))
 
-    far = [x for l in list(HELP) + list(OWN.values()) for x in l]
+    far = [x for l in HELP for x in l] + list(OWN)
     own_f, own_j = loaded(0, P), [("j1", 1)]
     j_tok = [own_j, own_j] + [[("aj%d" % s, NE)] for s in (2, 3)]
-    f_tok = [own_f, own_f] + [[("af%d" % s, NE * len([x for x in far if x[2] == s and x[0] >= 0]))] + j_tok[s] for s in (2, 3)]
-    u_tok = lambda s: ("au", NE) if s == GUEST else ("ldu", 16)
+    arrive = lambda s: [landed(*x) for x in far if x[2] == s]
+    f_tok = [own_f, own_f] + [[(k, NE * arrive(s).count(k)) for k in sorted(set(arrive(s)))] for s in (2, 3)]
+    u_tok = lambda n: ("au%d" % (n % NH), NE) if n // NH == GUEST else ("ldu", 16)
     n_tok = lambda s: ("an", NE) if s == GUEST else ("nk", NH)
     span = lambda n: (n // NH, CUT[n % NH], CUT[n % NH + 1], CUT[n % NH + 1] - CUT[n % NH])
     ps = lambda name, n: T[name + str(n % 2)]
-    through = lambda n: [c for c in range(4) if ROUTES[n // NH][c] != "V"]
-
-    def bank(c, n):
-        return "pb%d" % (n % 2) if c == 3 else "pa%d" % (n % 2 if len(through(n)) < 3 else c % 2)
-
-    formed = lambda c, n: ("b%d_%d" % (c, n % NH), len([m for m in range(n % NH, n + 1, NH) if c in through(m)]))
+    squared = lambda c, n: [tok("s%d" % c, n)] + ([tok("u2", n)] if c == 2 else [])
     k_in = lambda s, a, b: T.mg[:, 0, a:b] if s == GUEST else T.mo[:, s, a:b]
     k_out = lambda s, a, b: T.mg[:, 1, a:b] if s == GUEST else T.mo[:, s + 1, a:b]
 
@@ -212,49 +216,51 @@ def rank_program(g, core, T, topo):
         s = n // NH
         return ("lds", 16) if s == 0 else ("arr%d" % n, NE) if s in (GUEST, GUEST + 1) else tok("m4", n - NH)
 
-    last = float((rank + 3) % nr)
+    fr = [float((rank + s) % nr) for s in range(4)]
     ti = lambda k: T.ti[:, k, :]
+    tf = lambda k: T.tf[:, k, :]
+    keys = lambda s: [there((s + 1) * NH + h) for h in range(NH)]
 
-    def best(s, j):
-        m = T.mo[:, s + 1, :]
-        k = 4 * s - 4
-        if j == 0:
-            wait("V", ("t2", s - 1), *[there((s + 1) * NH + h) for h in range(NH)])
-            inc(V.tensor_scalar(T.ti[:, k:k + 2, :], T.mo[:, s:s + 2, :], -4097, None, ALU.bitwise_and), "t%d" % k)
-            if s == 2:
-                inc(V.tensor_scalar(ti(3), T.mo[:, 2, :], 12, 1, ALU.arith_shift_right, ALU.bitwise_and), "t3")
-        elif j == 1:
-            wait("V", ("t%d" % k, 1))
-            inc(V.tensor_scalar(ti(k + 2), ti(k + 1), 4096.0, None, ALU.add), "t%d" % (k + 1))
-        elif j == 2:
-            wait("V", ("t%d" % (k + 1), 1), *[tok("xy", (s + 1) * NH + h) for h in range(NH)])
-            inc(V.tensor_tensor(m, ti(k), ti(k + 2), ALU.min), "t%d" % (k + 2))
-        elif s < 2:
-            return
-        elif j == 3:
+    def best(i, j):
+        if (i, j) == (0, 0):
+            wait("V", *keys(1))
+            inc(V.tensor_scalar(T.ti[:, 0:2, :], T.mo[:, 1:3, :], -4097, None, ALU.bitwise_and), "t0")
+        elif (i, j) == (0, 1):
+            wait("V", ("t0", 1))
+            inc(V.tensor_scalar(ti(2), ti(1), 4096.0, None, ALU.add), "t1")
+        elif (i, j) == (0, 2):
+            wait("V", ("t1", 1))
+            inc(V.tensor_tensor(ti(3), ti(0), ti(2), ALU.min), "t2")
+        elif (i, j) == (1, 0):
+            wait("V", ("t2", 1))
+            inc(V.tensor_scalar(ti(6), ti(3), 12, 1, ALU.arith_shift_right, ALU.bitwise_and), "t3")
+            inc(V.tensor_scalar(ti(4), ti(3), -8192, None, ALU.bitwise_and), "t4")
+        elif (i, j) == (1, 1):
+            wait("V", ("t3", 1))
+            inc(V.tensor_scalar(tf(0), ti(6), fr[1] - fr[0], fr[0] - fr[2], ALU.mult, ALU.add), "t4")
+            inc(V.tensor_scalar(ti(5), ti(3), P - 1, None, ALU.bitwise_and), "t4")
+        elif (i, j) == (2, 0):
+            wait("V", ("t4", 3), *keys(2))
+            inc(V.tensor_tensor(ti(7), T.mo[:, 3, :], ti(4), ALU.min), "t5")
+            inc(V.tensor_tensor(tf(1), T.mo[:, 3, :], ti(4), ALU.is_ge), "t6")
+        elif (i, j) == (2, 1):
+            wait("V", ("t5", 1))
+            inc(V.tensor_scalar(ti(8), ti(7), -8192, None, ALU.bitwise_and), "t8")
+            inc(V.tensor_scalar(ti(10), ti(7), P - 1, None, ALU.bitwise_and), "t7")
             wait("V", ("t6", 1))
-            inc(V.tensor_scalar(ti(7), m, 11, 2, ALU.arith_shift_right, ALU.bitwise_and), "t7")
-            inc(V.tensor_scalar(ti(8), m, -8192, None, ALU.bitwise_and), "t11")
-        elif j == 4:
-            wait("V", ("t7", 1), ("t3", 1))
-            inc(V.tensor_tensor(ti(10), ti(3), ti(7), ALU.max), "t8")
-            inc(V.tensor_scalar(ti(9), m, P - 1, None, ALU.bitwise_and), "t11")
-        elif j == 5:
-            wait("V", ("t8", 1))
-            inc(V.tensor_scalar(ti(11), ti(10), float(rank), None, ALU.add), "t9")
-        elif j == 6:
-            wait("V", ("t9", 1))
-            inc(V.tensor_scalar(ti(12), ti(11), nr - 1, None, ALU.bitwise_and), "t10")
-        else:
-            wait("V", ("t10", 1))
-            inc(V.tensor_scalar(T.tf[:, 0, :], ti(12), -last, None, ALU.add), "t11")
+            inc(V.tensor_tensor(tf(2), tf(1), ti(5), ALU.mult), "t7")
+            inc(V.tensor_tensor(tf(3), tf(1), tf(0), ALU.mult), "t7")
+        elif (i, j) == (2, 2):
+            wait("V", ("t7", 3))
+            inc(V.tensor_tensor(ti(9), tf(2), ti(10), ALU.add), "t8")
+            inc(V.tensor_scalar(tf(4), tf(3), fr[2] - fr[3], None, ALU.add), "t8")
 
     def results(n, j):
         s, a, b, w = span(n)
         ft = lambda role: (role + "_" + str(n % NH), FIN[role])
-        m, thr, new, keep = T.mo[:, 4, a:b], T.ti[:, 8, a:b], T.ti[:, 13, a:b], T.tf[:, 1, a:b]
+        m, thr, new, keep = T.mo[:, 4, a:b], T.ti[:, 8, a:b], T.ti[:, 13, a:b], T.tf[:, 5, a:b]
         if j == 0:
-            wait("V", ("t11", 3), tok("m4", n))
+            wait("V", ("t8", 3), tok("m4", n))
             rinc(V.tensor_tensor(new, m, thr, ALU.min), "fn", n)
             rinc(V.tensor_tensor(keep, m, thr, ALU.is_ge), "fk", n)
         elif j == 1:
@@ -262,30 +268,35 @@ def rank_program(g, core, T, topo):
             rinc(V.tensor_scalar(T.ti[:, 14, a:b], new, 13, None, ALU.arith_shift_right), "fc", n)
             rinc(V.tensor_scalar(T.ti[:, 15, a:b], new, P - 1, None, ALU.bitwise_and), "fp", n)
             wait("V", ft("fk"))
-            rinc(V.tensor_tensor(T.tf[:, 3, a:b], keep, T.tf[:, 0, a:b], ALU.mult), "ff", n)
-            rinc(V.tensor_tensor(T.tf[:, 2, a:b], keep, T.ti[:, 9, a:b], ALU.mult), "fp", n)
+            rinc(V.tensor_tensor(T.tf[:, 7, a:b], keep, T.tf[:, 4, a:b], ALU.mult), "ff", n)
+            rinc(V.tensor_tensor(T.tf[:, 6, a:b], keep, T.ti[:, 9, a:b], ALU.mult), "fp", n)
         elif j == 2:
             wait("V", ft("fc"))
             rinc(V.tensor_scalar(T.oc[:, a:b], T.ti[:, 14, a:b], float(MID), None, ALU.add), "yc", n)
             if n == NN - 1:
                 wait("S", ft("ff"))
-                rinc(S.activation(T.of[:, a:b], T.tf[:, 3, a:b], ACT.Identity, bias=last), "yf", n)
+                rinc(S.activation(T.of[:, a:b], T.tf[:, 7, a:b], ACT.Identity, bias=fr[3]), "yf", n)
             else:
                 wait("V", ft("ff"))
-                rinc(V.tensor_scalar(T.of[:, a:b], T.tf[:, 3, a:b], last, None, ALU.add), "yf", n)
+                rinc(V.tensor_scalar(T.of[:, a:b], T.tf[:, 7, a:b], fr[3], None, ALU.add), "yf", n)
             wait("V", ft("fp"))
-            rinc(V.tensor_tensor(T.op[:, a:b], T.tf[:, 2, a:b], T.ti[:, 15, a:b], ALU.add), "yp", n)
+            rinc(V.tensor_tensor(T.op[:, a:b], T.tf[:, 6, a:b], T.ti[:, 15, a:b], ALU.add), "yp", n)
 
     def emit(e, stage, n):
         s, a, b, w = span(n)
         q = 16 * w
         u = T.ua[:, int(s == GUEST), 16 * a:16 * b]
-        ke, kl = ps("pc", n)[:, KE:KE + 2 * w], ps("pl", n)[:, 0:2 * w]
-        if stage[0] in "gsab" and stage[1:].isdigit():
-            c = int(stage[1])
-            k, route = POS[c], ROUTES[s][c]
-            gd, sq = T.gd[:, n, k * q:(k + 1) * q], T.sq[:, n, k * q:(k + 1) * q]
-            pb = T[bank(c, n)][:, 0:q]
+        ke, kl = ps("pc", n)[:, KE:KE + 2 * w], ps("pl", n)[:, KE:KE + 2 * w]
+        if stage[0] in "gstuab":
+            c = halved(n) if stage == "t" else int(stage[1])
+            k, route = POS[c], ROUTES[n][c]
+            lo, hi, step = 0, q, 1
+            if stage[0] in "st" and c == halved(n):
+                lo, step = int(stage == "t"), 2
+            elif stage in ("s2", "u2") and home(n):
+                lo, hi = (0, q // 2) if stage == "s2" else (q // 2, q)
+            gd, sq = T.gd[:, n, k * q + lo:k * q + hi:step], T.sq[:, n, k * q + lo:k * q + hi:step]
+            pb = ps("pb" if c == 3 else "pa", n)[:, lo:hi:step]
         if stage == "xy":
             wait("V", there(n))
             rinc(V.tensor_scalar(T.xyi[:, s, 0, a:b], k_in(s, a, b), 63, None, ALU.bitwise_and), "xy", n)
@@ -295,8 +306,9 @@ def rank_program(g, core, T, topo):
             src = T.xyi[:, s, :, a:b]
             rinc(V.tensor_copy(T.xyb[:, 4 * s:4 * s + 2, 2 + a:2 + b], src), "cv", n)
             rinc(V.tensor_scalar(T.xyb[:, 4 * s + 2:4 * s + 4, 2 + a:2 + b], src, 1.0, 63.0, ALU.add, ALU.min), "cv", n)
-        elif stage == "cc":
-            wait("PE", tok("cv", n), tok("cv", n - 1), tok("kc", n - 2), *j_tok[s])
+        elif stage in ("cc", "cd"):
+            late = int(stage == "cd")
+            wait("PE", tok("cv", n), tok("cv", n - 1), *([tok("m1", n - 2)] + j_tok[s] if late else [tok("kc", n - 2)]))
             pl = lambda k, d: T.xyb[:, 4 * s + k, 2 + a - d:2 + b - d]
             jp = lambda k: T.fa[:, SLOT[s], k * K + a:k * K + b]
             e1, e64 = T.eye[:], T.eye64[:]
@@ -304,56 +316,58 @@ def rank_program(g, core, T, topo):
                       [(e64, pl(3, 2)), (e1, pl(0, 2))],
                       [(T.sh[:, 1, :], pl(1, 0)), (T.sh[:, 0, :], pl(2, 0)), (T.wr[:, 1, :], pl(1, 1)), (T.wr[:, 0, :], pl(2, 1))],
                       [(e64, pl(1, 0)), (e1, pl(0, 0)), (e64, jp(0)), (e1, jp(1))]]
-            for k, grp in enumerate(groups):
+            for k, grp in enumerate(groups[2 * late:2 * late + 2]):
                 for j, (l, r) in enumerate(grp):
-                    ins = PE.matmul(ps("pc", n)[:, k * w:(k + 1) * w], l, r, j == 0, j == len(grp) - 1)
-                rinc(ins, "cc", n)
-        elif stage == "off":
-            wait("V", tok("cc", n))
-            rinc(V.tensor_scalar(T.off[:, n, 0:4 * w], ps("pc", n)[:, 0:4 * w], 0.0, float(P - 1), ALU.max, ALU.min), "off", n)
+                    ins = PE.matmul(ps(("pc", "pl")[late], n)[:, k * w:(k + 1) * w], l, r, j == 0, j == len(grp) - 1)
+            rinc(ins, stage, n)
+        elif stage in ("off", "of2"):
+            late = int(stage == "of2")
+            wait("V", tok(("cc", "cd")[late], n))
+            rinc(V.tensor_scalar(T.off[:, n, 2 * late * w:2 * (late + 1) * w], ps(("pc", "pl")[late], n)[:, 0:2 * w],
+                                 0.0, float(P - 1), ALU.max, ALU.min), stage, n)
         elif stage == "plc":
-            wait("V", tok("off", n))
+            wait("V", tok("off", n), tok("of2", n))
             rinc(V.tensor_scalar(T.plc[:, n, 0:4 * w], T.off[:, n, 0:4 * w], -2048.0, None, ALU.add), "plc", n)
         elif stage[0] == "g":
             win = T.fa[:, SLOT[s], J:J + P].indirect(T.off[:, n, k * w:(k + 1) * w])
-            wait(e, tok("off", n), *f_tok[s])
+            wait(e, tok("of2" if c % 2 else "off", n), *f_tok[s])
             if route == "V":
-                wait(e, u_tok(s))
+                wait(e, u_tok(n))
                 rinc(V.tensor_tensor(gd, win, u, ALU.subtract), stage, n)
             else:
                 rinc(S.activation(gd, win, ACT.Copy), stage, n)
         elif stage[0] == "a":
-            before = [tok("s%d" % x, m) for m in range(n) for x in through(m) if bank(x, m) == bank(c, n)]
-            wait("PE", u_tok(s), *before[-1:])
+            wait("PE", u_tok(n), tok("t", n - 2), *squared(c, n - 2))
             PE.matmul(pb, T.eyem[:, int(route == "M"), :], u, True, False)
         elif stage[0] == "b":
             wait("PE", tok("g%d" % c, n))
             rinc(PE.matmul(pb, T.eye[:], gd, False, True), stage, n)
-        elif stage[0] == "s":
-            wait(e, tok("g%d" % c, n) if route == "V" else formed(c, n))
+        elif stage[0] in "stu":
+            wait(e, tok(("g%d" if route == "V" else "b%d") % c, n))
             if route == "M":
                 rinc(V.tensor_tensor(sq, pb, gd, ALU.mult), stage, n)
             else:
                 rinc(S.activation(sq, gd if route == "V" else pb, ACT.Square), stage, n)
         elif stage == "pre":
-            wait("PE", tok("plc", n), tok("m1", n - 2), n_tok(s))
+            wait("PE", tok("plc", n), n_tok(s))
             for j, kk in enumerate((ke, kl)):
-                table = ROUTES[s][2 + j] == "M"
+                table = ROUTES[n][2 + j] == "M"
                 PE.matmul(kk, T.eyeh[:], T.plc[:, n, 2 * j * w:2 * (j + 1) * w], True, False)
                 PE.matmul(kk, T.cl[0:65, :], T.ct[0:65, n % NH + (0 if table else NH), j, 0:2 * w], False, False)
                 if table:
                     PE.matmul(kk, T.eyek[:], T.nq[:, int(s == GUEST), 2 * a:2 * b], False, False)
-        elif stage in ("ke", "kl"):
-            j = int(stage == "kl")
-            wait("PE", tok("s%d" % j, n), tok("s%d" % (2 + j), n))
-            for r in range(16):
+        elif stage in ("ke", "kl", "km"):
+            j = int(stage != "ke")
+            wait("PE", *([tok("t", n)] if stage == "km" else squared(j, n) + squared(2 + j, n)))
+            for r in {"ke": range(16), "kl": range(0, 16, 2), "km": range(1, 16, 2)}[stage]:
                 ins = PE.matmul((ke, kl)[j], T.sel[:, 15 - r:143 - r], T.sq[:, n, 2 * j * q + r:2 * (j + 1) * q:16], False, r == 15)
-            rinc(ins, stage, n)
+            if stage != "kl":
+                rinc(ins, stage, n)
         elif stage == "kc":
             wait("S", tok("ke", n))
             rinc(S.activation(T.kec[:, n, 0:2 * w], ke, ACT.Copy), "kc", n)
         elif stage == "m1":
-            wait("V", tok("kc", n), tok("kl", n))
+            wait("V", tok("kc", n), tok("km", n))
             rinc(V.tensor_tensor(T.ab[:, n, 0:2 * w], kl, T.kec[:, n, 0:2 * w], ALU.min), "m1", n)
         elif stage == "m2":
             wait("V", tok("m1", n))
@@ -364,10 +378,13 @@ def rank_program(g, core, T, topo):
         elif stage == "m4":
             wait("V", tok("m3", n))
             rinc(V.tensor_tensor(k_out(s, a, b), T.abc[:, n, 0:w], T.bs[:, n, 0:w], ALU.min), "m4", n)
-        elif stage[0] == "q" and n in BEST_AT:
-            best(BEST_AT[n], int(stage[1]))
-        elif stage[0] == "q" and n > NN - NH:
+        elif stage[0] == "q" and n < NN - 1:
+            best(n - 2 * NH, int(stage[1]))
+        elif stage[0] == "q":
             results(n - 1, int(stage[1]))
+
+    def runs_on(e, stage, n):
+        return stage[0] != "s" or (e == "V") == (ROUTES[n][int(stage[1])] == "M")
 
     for n in range(NH):
         emit("V", "xy", n)
@@ -378,48 +395,57 @@ def rank_program(g, core, T, topo):
         emit("V", "cv", n)
     wait("V", ("j0", 2))
     inc(V.tensor_copy(T.fa[:, 0, 0:J], T.jint[:]), "j1")
+    for e, stages in (("PE", ("cc", "cd")), ("V", ("off", "of2"))):
+        for n in range(NH):
+            for stage in stages:
+                emit(e, stage, n)
+    for n in range(NH):
+        emit("V", "plc", n)
     wait("S", ("ldu", 16))
     inc(S.activation(T.usq[:], T.ua[:, 0, :], ACT.Square), "us")
     wait("PE", ("us", 1))
     for r in range(16):
-        ins = PE.matmul(T.pl1[:, 0:K], T.sel[:, 15 - r:143 - r], T.usq[:, r:Q:16], r == 0, r == 15)
+        ins = PE.matmul(T.pb1[:, 0:K], T.sel[:, 15 - r:143 - r], T.usq[:, r:Q:16], r == 0, r == 15)
     inc(ins, "nu")
     wait("V", ("nu", 1))
     for h in range(NH):
         s, a, b, w = span(h)
-        inc(V.tensor_scalar(T.nq[:, 0, 2 * a + w:2 * b], T.pl1[:, a:b], 1.0 / 8192, -float(MID), ALU.mult, ALU.add), "nk")
-    for n in range(NH):
-        emit("PE", "cc", n)
-        emit("V", "off", n)
-    for n in range(NH):
-        emit("V", "plc", n)
+        inc(V.tensor_scalar(T.nq[:, 0, 2 * a + w:2 * b], T.pb1[:, a:b], 1.0 / 8192, -float(MID), ALU.mult, ALU.add), "nk")
 
-    done = [(stage, n) for stage in ("xy", "cv", "cc", "off", "plc") for n in range(NH)]
+    done = [(stage, n) for stage in ("xy", "cv", "cc", "cd", "off", "of2", "plc") for n in range(NH)]
     for e in ("V", "S", "PE"):
         for i in range(NN + 1):
-            for stage, d in (AWAY if i < (GUEST + 1) * NH else HOME)[e]:
-                if 0 <= i + d < NN and (stage, i + d) not in done:
+            for stage, d in (HOME if home(i) else AWAY if i else FIRST)[e]:
+                if 0 <= i + d < NN and (stage, i + d) not in done and runs_on(e, stage, i + d) and (stage[0] != "q" or home(i + d)):
                     done.append((stage, i + d))
                     emit(e, stage, i + d)
     for j in range(3):
         results(NN - 1, j)
 
-    sent = 0
+    hs, near = helpers_of(T, topo, rank), near_engines(T, topo, rank)
+    queries = lambda h: write(g, T, topo, peer(1), T.ua[:, 1, 16 * CUT[h]:16 * CUT[h + 1]],
+                              T.ua[:, 0, 16 * CUT[h]:16 * CUT[h + 1]], "au%d" % h, topo.engines(core, peer(1)))
+    wait("G", ("ldu", 16))
+    sent = queries(0)
     wait("G", ("nk", NH), ("c10", 3))
     sent += write(g, T, topo, peer(1), T.nq[:, 1, :], T.nq[:, 0, :], "an", topo.engines(core, peer(1)))
-    wait("G", ("ldu", 16), *own_f)
-    sent += write(g, T, topo, peer(1), T.ua[:, 1, :], T.ua[:, 0, :], "au", topo.engines(core, peer(1)))
+    wait("G", *own_f)
     for k, (a, b, h) in enumerate(FEEDS):
-        wait("G", *loaded(a, b))
         part = T.fa[:, 0, J + a:J + b]
-        sent += write(g, T, topo, helpers_of(T, topo, rank)[h], part, part, "hp%d" % k, near_engines(T, topo, rank))
+        sent += write(g, T, topo, hs[h], part, part, "hp%d" % k, near)
     for n in range((GUEST + 1) * NH):
         s, a, b, w = span(n)
         dst = peer(-1 if s == GUEST else 1)
         wait("G", tok("m4", n))
         sent += write(g, T, topo, dst, k_in(s + 1, a, b), k_out(s, a, b), "arr%d" % (n + NH), topo.engines(core, dst))
-        for x in OWN.get(n, ()):
-            sent += hand_on(g, core, T, topo, rank, *x)
+        if n + 1 < NH:
+            sent += queries(n + 1)
+        a, b, s = OWN[n]
+        if s == 3 and not topo.mates(topo.chip(core), topo.chip(peer(-s))):
+            wait("G", *[t for t in f_tok[2] if b > OWN[1][1] or t[0] != "af2"])
+            sent += hand_on(g, core, T, topo, (rank + 2) % nr, a, b, s, SLOT[2])
+        else:
+            sent += hand_on(g, core, T, topo, rank, a, b, s)
     total["sent"] = sent
 
     for q, out, src in (("SY", "yc", T.oc), ("S", "yf", T.of), ("SY", "yp", T.op)):

@@ -15,21 +15,25 @@ SLOT = (0, 0, 1, 2)
 ROUTES = ["VVMM"] * 4 + ["VVMS"] * 3 + ["VVMM"]
 POS = (0, 2, 1, 3)
 
-LOADS = ("u", (0, P))
-OWN = ((-J, 512, 2), (512, 1536, 2), (-J, 896, 3), (896, 2176, 3))
-FEEDS = ((2176, 2816, 1), (1536, 2176, 0), (2816, 3456, 1), (3456, P, 0))
+OWN = ((-J, 640, 2), (640, 1664, 2), (-J, 896, 3), (896, 2176, 3))
+FEEDS = ((1664, 2176, 0), (2176, 2816, 1), (3392, P, 0), (2816, 3392, 1))
 HELP = [[(a, b, s) for s in (2, 3) for a, b, x in FEEDS if x == h and (s == 2 or a >= OWN[3][1])] for h in range(2)]
 
-AWAY = {"V": [("g0", 0), ("g1", 0), ("s2", 0), ("s3", 0), ("xy", 1), ("cv", 1),
-              ("m1", 0), ("m2", 0), ("off", 1), ("of2", 1), ("m3", 0), ("plc", 1), ("m4", 0)],
-        "S": [("g2", 0), ("g3", 0), ("s0", 0), ("s1", 0), ("t", 0), ("kc", 0)],
-        "PE": [("a2", 0), ("a3", 0), ("b2", 0), ("pre", 0), ("b3", 0), ("a2", 1), ("ke", 0), ("kl", 0), ("km", 0),
+AWAY = {"V": [("g0", 0), ("g1", 0), ("s2", 0), ("t2", 0), ("s3", 0), ("t3", 0), ("xy", 1), ("px", 1), ("cv", 1), ("pu", 1),
+              ("m1", 0), ("m2", 0), ("off", 1), ("m3", 0), ("of2", 1), ("m4", 0), ("g0", 1), ("plc", 1)],
+        "S": [("g2", 0), ("g3", 0), ("s0", 0), ("t0", 0), ("s1", 0), ("t1", 0), ("kc", 0)],
+        "PE": [("a2", 0), ("a3", 0), ("b2", 0), ("pre", 0), ("b3", 0), ("a2", 1), ("ke", 0), ("kf", 0), ("kl", 0), ("km", 0),
                ("cc", 1), ("cd", 1), ("a3", 1)]}
-FIRST = dict(AWAY, V=AWAY["V"][:4] + [("g0", 1)] + AWAY["V"][4:])
-HOME = {"V": [("g0", 0), ("m1", -1), ("plc", 0), ("q2", -1), ("m2", -1), ("g1", 0), ("m3", -1), ("s2", 0), ("m4", -1),
-              ("u2", 0), ("s3", 0), ("xy", 1), ("q0", 0), ("cv", 1), ("q1", 0), ("off", 1), ("of2", 1)],
-        "S": [("g2", 0), ("g3", 0), ("s0", 0), ("s1", 0), ("s3", 0), ("t", 0), ("kc", 0)],
-        "PE": [("b2", 0), ("a3", 1), ("b3", 0), ("pre", 0), ("a2", 1), ("ke", 0), ("cc", 1), ("cd", 1), ("kl", 0), ("km", 0)]}
+FIRST = {"V": AWAY["V"][:6] + [("g0", 1), ("m1", 0), ("m2", 0), ("m3", 0), ("nk", 1), ("m4", 0)],
+         "S": AWAY["S"][:-1] + [("us", 1), ("kc", 0)], "PE": AWAY["PE"][:-1] + [("nu", 1), ("a3", 1)]}
+HOME = {"V": [("g0", 0), ("m1", -1), ("of2", 0), ("q2", -1), ("m2", -1), ("plc", 0), ("g1", 0), ("m3", -1), ("s2", 0),
+              ("m4", -1), ("t2", 0), ("xy", 1), ("px", 1), ("q0", 0), ("cv", 1), ("pu", 1), ("q1", 0), ("off", 1)],
+        "S": [("g2", 0), ("g3", 0), ("s0", 0), ("t0", 0), ("s1", 0), ("t1", 0), ("s3", 0), ("t3", 0), ("kc", 0)],
+        "PE": [("a3", 0), ("b2", 0), ("pre", 0), ("a2", 1), ("b3", 0), ("ke", 0), ("kf", 0), ("cc", 1), ("cd", 1),
+               ("kl", 0), ("km", 0)]}
+LAST = dict(HOME, V=[("g0", 0), ("of2", 0), ("m1", -1), ("q2", -1), ("plc", 0), ("g1", 0), ("m2", -1), ("s2", 0), ("m3", -1),
+                     ("t2", 0), ("s3", 0), ("m4", -1), ("t3", 0), ("q0", 0), ("q1", 0), ("q2", 0), ("m1", 0), ("m2", 0),
+                     ("z0", 0), ("m3", 0), ("z1", 0), ("z2", 0), ("z3", 0), ("z4", 0)])
 
 SCRATCH = {
     "fa": ("sbuf", [128, 3, J + P], "bfloat16"),
@@ -37,7 +41,7 @@ SCRATCH = {
     "nq": ("sbuf", [128, 2, NH * 2 * W], HALF),
     "jraw": ("sbuf", [128, K], "int32"), "jint": ("sbuf", [128, 2 * K], "int32"),
     "mo": ("sbuf", [128, 5, K], "int32"), "mg": ("sbuf", [128, 2, K], "int32"),
-    "xyi": ("sbuf", [128, 4, 2, K], "int32"), "xyb": ("sbuf", [128, 16, K + 2], "bfloat16"),
+    "xyi": ("sbuf", [128, 4, 3, K], "int32"), "xyb": ("sbuf", [128, 16, K + 2], "bfloat16"),
     "off": ("sbuf", [128, NN, 4 * W], "uint16"), "plc": ("sbuf", [128, NN, 4 * W], HALF),
     "gd": ("sbuf", [128, NN, 64 * W], "bfloat16"), "sq": ("sbuf", [128, NN, 64 * W], "bfloat16"),
     "kec": ("sbuf", [128, NN, 2 * W], "float32"), "ab": ("sbuf", [128, NN, 2 * W], "int32"),
@@ -57,14 +61,14 @@ for _h in range(2):
 KE = 256
 
 ROLES = {"xy": 2, "cv": 2, "cc": 1, "cd": 1, "off": 1, "of2": 1, "plc": 1, "g0": 1, "g1": 1, "g2": 1, "g3": 1,
-         "s0": 1, "s1": 1, "s2": 1, "s3": 1, "t": 1, "u2": 1, "b2": 1, "b3": 1, "ke": 1, "km": 1, "kc": 1,
-         "m1": 1, "m2": 1, "m3": 1, "m4": 1}
+         "s0": 1, "s1": 1, "s2": 1, "s3": 1, "t0": 1, "t1": 1, "t2": 1, "t3": 1, "px": 1, "pu": 1, "b2": 1, "b3": 1,
+         "kf": 1, "km": 1, "kc": 1, "m1": 1, "m2": 1, "m3": 1, "m4": 1}
 FIN = {"fn": 1, "fk": 1, "fc": 1, "fp": 2, "ff": 1, "yc": 1, "yp": 1, "yf": 1}
 SEMAPHORES = ([r + "_" + str(h) for r in list(ROLES) + list(FIN) for h in range(NH)]
-              + ["ldf%d" % k for k in range(len(LOADS))] + ["hp%d" % k for k in range(len(FEEDS))]
+              + ["hp%d" % k for k in range(len(FEEDS))] + [a + str(h) for a in ("ldu", "us", "nu", "nk", "au") for h in range(NH)]
               + ["arr%d" % n for n in range(NH, 3 * NH)] + [a + str(k) for a in ("af", "aj") for k in (2, 3)]
               + [a + str(k) for a in "tc" for k in range(12)]
-              + ["ldu", "lds", "ldj", "sty", "sent", "j0", "j1", "us", "nu", "nk", "an", "ag"] + ["au%d" % h for h in range(NH)])
+              + ["ldf", "lds", "ldj", "sty", "sent", "j0", "j1", "an", "ag"])
 
 
 def mask_of(engs):
@@ -136,10 +140,10 @@ def rank_program(g, core, T, topo):
         total[name] = total.get(name, 0) + k
 
     home = lambda n: n >= (GUEST + 1) * NH
-    halved = lambda n: 3 if ROUTES[n][3] == "S" else 1
+    has = lambda role, n: home(n) or role not in ("px", "pu") and role[0] != "q"
 
     def tok(role, n):
-        return (role + "_" + str(n % NH), ROLES[role] * len([m for m in range(n % NH, n + 1, NH) if role != "u2" or home(m)]))
+        return (role + "_" + str(n % NH), ROLES[role] * len([m for m in range(n % NH, n + 1, NH) if has(role, m)]))
 
     def rinc(ins, role, n):
         inc(ins, role + "_" + str(n % NH))
@@ -149,12 +153,10 @@ def rank_program(g, core, T, topo):
 
     inc(S.dma_start(T.mo[:, 0, :], T.st[:]), "lds", 16)
     inc(S.dma_start(T.jraw[:], T.ju[:]), "ldj", 16)
-    for k, x in enumerate(LOADS):
-        if x == "u":
-            inc(SY.dma_start(T.ua[:, 0, :], T.qu[:]), "ldu", 16)
-        else:
-            inc(SY.dma_start(T.fa[:, 0, J + x[0]:J + x[1]], T.fr[:, x[0]:x[1]]), "ldf%d" % k, 16)
-    loaded = lambda a, b: [("ldf%d" % k, 16) for k, x in enumerate(LOADS) if x != "u" and x[0] < b and a < x[1]]
+    for h in range(NH):
+        inc(SY.dma_start(T.ua[:, 0, 16 * CUT[h]:16 * CUT[h + 1]], T.qu[:, 16 * CUT[h]:16 * CUT[h + 1]]), "ldu%d" % h, 16)
+        if h == 0:
+            inc(SY.dma_start(T.fa[:, 0, J:J + P], T.fr[:]), "ldf", 16)
 
     inc(V.memset(T.ones[:], 1.0), "c0")
     inc(V.memset(T.wr[:], 0.0), "c1")
@@ -200,15 +202,14 @@ def rank_program(g, core, T, topo):
     wait("PE", ("c7", total["c7"]), ("c1", 4), ("c5", 4), ("c6", 3), ("c2", 1))
 
     far = [x for l in HELP for x in l] + list(OWN)
-    own_f, own_j = loaded(0, P), [("j1", 1)]
+    own_f, own_j = [("ldf", 16)], [("j1", 1)]
     j_tok = [own_j, own_j] + [[("aj%d" % s, NE)] for s in (2, 3)]
     arrive = lambda s: [landed(*x) for x in far if x[2] == s]
     f_tok = [own_f, own_f] + [[(k, NE * arrive(s).count(k)) for k in sorted(set(arrive(s)))] for s in (2, 3)]
-    u_tok = lambda n: ("au%d" % (n % NH), NE) if n // NH == GUEST else ("ldu", 16)
-    n_tok = lambda s: ("an", NE) if s == GUEST else ("nk", NH)
+    u_tok = lambda n: ("au%d" % (n % NH), NE) if n // NH == GUEST else ("ldu%d" % (n % NH), 16)
+    n_tok = lambda n: ("an", NE) if n // NH == GUEST else ("nk%d" % (n % NH), 1)
     span = lambda n: (n // NH, CUT[n % NH], CUT[n % NH + 1], CUT[n % NH + 1] - CUT[n % NH])
     ps = lambda name, n: T[name + str(n % 2)]
-    squared = lambda c, n: [tok("s%d" % c, n)] + ([tok("u2", n)] if c == 2 else [])
     k_in = lambda s, a, b: T.mg[:, 0, a:b] if s == GUEST else T.mo[:, s, a:b]
     k_out = lambda s, a, b: T.mg[:, 1, a:b] if s == GUEST else T.mo[:, s + 1, a:b]
 
@@ -273,37 +274,81 @@ def rank_program(g, core, T, topo):
         elif j == 2:
             wait("V", ft("fc"))
             rinc(V.tensor_scalar(T.oc[:, a:b], T.ti[:, 14, a:b], float(MID), None, ALU.add), "yc", n)
-            if n == NN - 1:
-                wait("S", ft("ff"))
-                rinc(S.activation(T.of[:, a:b], T.tf[:, 7, a:b], ACT.Identity, bias=fr[3]), "yf", n)
-            else:
-                wait("V", ft("ff"))
-                rinc(V.tensor_scalar(T.of[:, a:b], T.tf[:, 7, a:b], fr[3], None, ALU.add), "yf", n)
+            wait("V", ft("ff"))
+            rinc(V.tensor_scalar(T.of[:, a:b], T.tf[:, 7, a:b], fr[3], None, ALU.add), "yf", n)
             wait("V", ft("fp"))
             rinc(V.tensor_tensor(T.op[:, a:b], T.tf[:, 6, a:b], T.ti[:, 15, a:b], ALU.add), "yp", n)
+
+    def last_results(n, j):
+        s, a, b, w = span(n)
+        ft = lambda role: (role + "_" + str(n % NH), FIN[role])
+        thr, low, new, keep = T.ti[:, 8, a:b], T.ti[:, 12, a:b], T.ti[:, 13, a:b], T.tf[:, 5, a:b]
+        if j == 0:
+            wait("V", ("t8", 3), tok("m1", n))
+            for k in range(2):
+                inc(V.tensor_tensor(T.tf[:, k, a:b], T.ab[:, n, k * w:(k + 1) * w], thr, ALU.is_ge), "t9")
+        elif j == 1:
+            wait("V", tok("m2", n))
+            inc(V.tensor_tensor(low, T.abc[:, n, 0:w], thr, ALU.min), "t10")
+            wait("V", ("t9", 2))
+            rinc(V.tensor_tensor(keep, T.tf[:, 0, a:b], T.tf[:, 1, a:b], ALU.mult), "fk", n)
+        elif j == 2:
+            wait("V", ("t10", 1), tok("m3", n))
+            rinc(V.tensor_tensor(new, low, T.bs[:, n, 0:w], ALU.min), "fn", n)
+            wait("V", ft("fk"))
+            rinc(V.tensor_tensor(T.tf[:, 7, a:b], keep, T.tf[:, 4, a:b], ALU.mult), "ff", n)
+            rinc(V.tensor_tensor(T.tf[:, 6, a:b], keep, T.ti[:, 9, a:b], ALU.mult), "fp", n)
+        elif j == 3:
+            wait("V", ft("fn"))
+            rinc(V.tensor_scalar(T.ti[:, 15, a:b], new, P - 1, None, ALU.bitwise_and), "fp", n)
+            rinc(V.tensor_scalar(T.ti[:, 14, a:b], new, 13, None, ALU.arith_shift_right), "fc", n)
+            wait("V", ft("ff"))
+            rinc(V.tensor_scalar(T.of[:, a:b], T.tf[:, 7, a:b], fr[3], None, ALU.add), "yf", n)
+        else:
+            wait("V", ft("fp"))
+            rinc(V.tensor_tensor(T.op[:, a:b], T.tf[:, 6, a:b], T.ti[:, 15, a:b], ALU.add), "yp", n)
+            wait("V", ft("fc"))
+            rinc(V.tensor_scalar(T.oc[:, a:b], T.ti[:, 14, a:b], float(MID), None, ALU.add), "yc", n)
 
     def emit(e, stage, n):
         s, a, b, w = span(n)
         q = 16 * w
         u = T.ua[:, int(s == GUEST), 16 * a:16 * b]
         ke, kl = ps("pc", n)[:, KE:KE + 2 * w], ps("pl", n)[:, KE:KE + 2 * w]
-        if stage[0] in "gstuab":
-            c = halved(n) if stage == "t" else int(stage[1])
+        if stage == "us":
+            wait("S", u_tok(n))
+            inc(S.activation(T.usq[:, 16 * a:16 * b], u, ACT.Square), "us%d" % n)
+            return
+        if stage == "nu":
+            wait("PE", ("us%d" % n, 1), tok("of2", n))
+            for r in range(16):
+                ins = PE.matmul(ps("pl", n)[:, 2 * w:3 * w], T.sel[:, 15 - r:143 - r], T.usq[:, 16 * a + r:16 * b:16], r == 0, r == 15)
+            inc(ins, "nu%d" % n)
+            return
+        if stage == "nk":
+            wait("V", ("nu%d" % n, 1))
+            inc(V.tensor_scalar(T.nq[:, 0, 2 * a + w:2 * b], ps("pl", n)[:, 2 * w:3 * w], 1.0 / 8192, -float(MID), ALU.mult, ALU.add),
+                "nk%d" % n)
+            return
+        if stage[0] in "gstab":
+            c = int(stage[1])
             k, route = POS[c], ROUTES[n][c]
-            lo, hi, step = 0, q, 1
-            if stage[0] in "st" and c == halved(n):
-                lo, step = int(stage == "t"), 2
-            elif stage in ("s2", "u2") and home(n):
-                lo, hi = (0, q // 2) if stage == "s2" else (q // 2, q)
-            gd, sq = T.gd[:, n, k * q + lo:k * q + hi:step], T.sq[:, n, k * q + lo:k * q + hi:step]
-            pb = ps("pb" if c == 3 else "pa", n)[:, lo:hi:step]
+            lo, step = {"s": (0, 2), "t": (1, 2)}.get(stage[0], (0, 1))
+            gd, sq = T.gd[:, n, k * q + lo:(k + 1) * q:step], T.sq[:, n, k * q + lo:(k + 1) * q:step]
+            pb = ps("pb" if c == 3 else "pa", n)[:, lo:q:step]
         if stage == "xy":
             wait("V", there(n))
             rinc(V.tensor_scalar(T.xyi[:, s, 0, a:b], k_in(s, a, b), 63, None, ALU.bitwise_and), "xy", n)
             rinc(V.tensor_scalar(T.xyi[:, s, 1, a:b], k_in(s, a, b), 6, 63, ALU.arith_shift_right, ALU.bitwise_and), "xy", n)
+        elif stage == "px":
+            wait("V", there(n))
+            rinc(V.tensor_scalar(T.xyi[:, s, 2, a:b], k_in(s, a, b), P - 1, None, ALU.bitwise_and), "px", n)
+        elif stage == "pu":
+            wait("V", tok("px", n))
+            rinc(V.tensor_copy(T.off[:, n, 0:w], T.xyi[:, s, 2, a:b]), "pu", n)
         elif stage == "cv":
             wait("V", tok("xy", n), ("c1", 4))
-            src = T.xyi[:, s, :, a:b]
+            src = T.xyi[:, s, 0:2, a:b]
             rinc(V.tensor_copy(T.xyb[:, 4 * s:4 * s + 2, 2 + a:2 + b], src), "cv", n)
             rinc(V.tensor_scalar(T.xyb[:, 4 * s + 2:4 * s + 4, 2 + a:2 + b], src, 1.0, 63.0, ALU.add, ALU.min), "cv", n)
         elif stage in ("cc", "cd"):
@@ -317,54 +362,55 @@ def rank_program(g, core, T, topo):
                       [(T.sh[:, 1, :], pl(1, 0)), (T.sh[:, 0, :], pl(2, 0)), (T.wr[:, 1, :], pl(1, 1)), (T.wr[:, 0, :], pl(2, 1))],
                       [(e64, pl(1, 0)), (e1, pl(0, 0)), (e64, jp(0)), (e1, jp(1))]]
             for k, grp in enumerate(groups[2 * late:2 * late + 2]):
-                for j, (l, r) in enumerate(grp):
+                for j, (l, r) in enumerate(grp if late or k or not home(n) else ()):
                     ins = PE.matmul(ps(("pc", "pl")[late], n)[:, k * w:(k + 1) * w], l, r, j == 0, j == len(grp) - 1)
             rinc(ins, stage, n)
         elif stage in ("off", "of2"):
             late = int(stage == "of2")
             wait("V", tok(("cc", "cd")[late], n))
-            rinc(V.tensor_scalar(T.off[:, n, 2 * late * w:2 * (late + 1) * w], ps(("pc", "pl")[late], n)[:, 0:2 * w],
+            lo = w if home(n) and not late else 0
+            rinc(V.tensor_scalar(T.off[:, n, 2 * late * w + lo:2 * (late + 1) * w], ps(("pc", "pl")[late], n)[:, lo:2 * w],
                                  0.0, float(P - 1), ALU.max, ALU.min), stage, n)
         elif stage == "plc":
-            wait("V", tok("off", n), tok("of2", n))
+            wait("V", tok("off", n), tok("of2", n), tok("pu", n))
             rinc(V.tensor_scalar(T.plc[:, n, 0:4 * w], T.off[:, n, 0:4 * w], -2048.0, None, ALU.add), "plc", n)
         elif stage[0] == "g":
             win = T.fa[:, SLOT[s], J:J + P].indirect(T.off[:, n, k * w:(k + 1) * w])
-            wait(e, tok("of2" if c % 2 else "off", n), *f_tok[s])
+            wait(e, tok("of2" if c % 2 else "pu" if c == 0 and home(n) else "off", n), *f_tok[s])
             if route == "V":
                 wait(e, u_tok(n))
                 rinc(V.tensor_tensor(gd, win, u, ALU.subtract), stage, n)
             else:
                 rinc(S.activation(gd, win, ACT.Copy), stage, n)
         elif stage[0] == "a":
-            wait("PE", u_tok(n), tok("t", n - 2), *squared(c, n - 2))
+            wait("PE", u_tok(n), tok("s%d" % c, n - 2), tok("t%d" % c, n - 2))
             PE.matmul(pb, T.eyem[:, int(route == "M"), :], u, True, False)
         elif stage[0] == "b":
             wait("PE", tok("g%d" % c, n))
             rinc(PE.matmul(pb, T.eye[:], gd, False, True), stage, n)
-        elif stage[0] in "stu":
+        elif stage[0] in "st":
             wait(e, tok(("g%d" if route == "V" else "b%d") % c, n))
             if route == "M":
                 rinc(V.tensor_tensor(sq, pb, gd, ALU.mult), stage, n)
             else:
                 rinc(S.activation(sq, gd if route == "V" else pb, ACT.Square), stage, n)
         elif stage == "pre":
-            wait("PE", tok("plc", n), n_tok(s))
+            wait("PE", tok("plc", n), n_tok(n))
             for j, kk in enumerate((ke, kl)):
                 table = ROUTES[n][2 + j] == "M"
                 PE.matmul(kk, T.eyeh[:], T.plc[:, n, 2 * j * w:2 * (j + 1) * w], True, False)
                 PE.matmul(kk, T.cl[0:65, :], T.ct[0:65, n % NH + (0 if table else NH), j, 0:2 * w], False, False)
                 if table:
                     PE.matmul(kk, T.eyek[:], T.nq[:, int(s == GUEST), 2 * a:2 * b], False, False)
-        elif stage in ("ke", "kl", "km"):
-            j = int(stage != "ke")
-            wait("PE", *([tok("t", n)] if stage == "km" else squared(j, n) + squared(2 + j, n)))
-            for r in {"ke": range(16), "kl": range(0, 16, 2), "km": range(1, 16, 2)}[stage]:
+        elif stage in ("ke", "kf", "kl", "km"):
+            j, odd = int(stage in ("kl", "km")), int(stage in ("kf", "km"))
+            wait("PE", tok("st"[odd] + str(j), n), tok("st"[odd] + str(2 + j), n))
+            for r in range(odd, 16, 2):
                 ins = PE.matmul((ke, kl)[j], T.sel[:, 15 - r:143 - r], T.sq[:, n, 2 * j * q + r:2 * (j + 1) * q:16], False, r == 15)
-            if stage != "kl":
+            if odd:
                 rinc(ins, stage, n)
         elif stage == "kc":
-            wait("S", tok("ke", n))
+            wait("S", tok("kf", n))
             rinc(S.activation(T.kec[:, n, 0:2 * w], ke, ACT.Copy), "kc", n)
         elif stage == "m1":
             wait("V", tok("kc", n), tok("km", n))
@@ -382,9 +428,11 @@ def rank_program(g, core, T, topo):
             best(n - 2 * NH, int(stage[1]))
         elif stage[0] == "q":
             results(n - 1, int(stage[1]))
+        elif stage[0] == "z":
+            last_results(n, int(stage[1]))
 
     def runs_on(e, stage, n):
-        return stage[0] != "s" or (e == "V") == (ROUTES[n][int(stage[1])] == "M")
+        return stage[0] not in "st" or (e == "V") == (ROUTES[n][int(stage[1])] == "M")
 
     for n in range(NH):
         emit("V", "xy", n)
@@ -401,35 +449,24 @@ def rank_program(g, core, T, topo):
                 emit(e, stage, n)
     for n in range(NH):
         emit("V", "plc", n)
-    wait("S", ("ldu", 16))
-    inc(S.activation(T.usq[:], T.ua[:, 0, :], ACT.Square), "us")
-    wait("PE", ("us", 1))
-    for r in range(16):
-        ins = PE.matmul(T.pb1[:, 0:K], T.sel[:, 15 - r:143 - r], T.usq[:, r:Q:16], r == 0, r == 15)
-    inc(ins, "nu")
-    wait("V", ("nu", 1))
-    for h in range(NH):
-        s, a, b, w = span(h)
-        inc(V.tensor_scalar(T.nq[:, 0, 2 * a + w:2 * b], T.pb1[:, a:b], 1.0 / 8192, -float(MID), ALU.mult, ALU.add), "nk")
+    for e, stage in (("S", "us"), ("PE", "nu"), ("V", "nk")):
+        emit(e, stage, 0)
 
     done = [(stage, n) for stage in ("xy", "cv", "cc", "cd", "off", "of2", "plc") for n in range(NH)]
     for e in ("V", "S", "PE"):
-        for i in range(NN + 1):
-            for stage, d in (HOME if home(i) else AWAY if i else FIRST)[e]:
-                if 0 <= i + d < NN and (stage, i + d) not in done and runs_on(e, stage, i + d) and (stage[0] != "q" or home(i + d)):
+        for i in range(NN):
+            for stage, d in (LAST if i == NN - 1 else HOME if home(i) else AWAY if i else FIRST)[e]:
+                if 0 <= i + d < NN and (stage, i + d) not in done and runs_on(e, stage, i + d) and has(stage, i + d):
                     done.append((stage, i + d))
                     emit(e, stage, i + d)
-    for j in range(3):
-        results(NN - 1, j)
 
     hs, near = helpers_of(T, topo, rank), near_engines(T, topo, rank)
     queries = lambda h: write(g, T, topo, peer(1), T.ua[:, 1, 16 * CUT[h]:16 * CUT[h + 1]],
                               T.ua[:, 0, 16 * CUT[h]:16 * CUT[h + 1]], "au%d" % h, topo.engines(core, peer(1)))
-    wait("G", ("ldu", 16))
+    wait("G", u_tok(0))
     sent = queries(0)
-    wait("G", ("nk", NH), ("c10", 3))
-    sent += write(g, T, topo, peer(1), T.nq[:, 1, :], T.nq[:, 0, :], "an", topo.engines(core, peer(1)))
-    wait("G", *own_f)
+    wait("G", *own_f, *own_j)
+    sent += hand_on(g, core, T, topo, rank, *OWN[0])
     for k, (a, b, h) in enumerate(FEEDS):
         part = T.fa[:, 0, J + a:J + b]
         sent += write(g, T, topo, hs[h], part, part, "hp%d" % k, near)
@@ -438,8 +475,11 @@ def rank_program(g, core, T, topo):
         dst = peer(-1 if s == GUEST else 1)
         wait("G", tok("m4", n))
         sent += write(g, T, topo, dst, k_in(s + 1, a, b), k_out(s, a, b), "arr%d" % (n + NH), topo.engines(core, dst))
-        if n + 1 < NH:
-            sent += queries(n + 1)
+        if n == 0:
+            wait("G", ("c10", 3), u_tok(1), *[n_tok(h) for h in range(NH)])
+            sent += write(g, T, topo, peer(1), T.nq[:, 1, :], T.nq[:, 0, :], "an", topo.engines(core, peer(1)))
+            sent += queries(1)
+            continue
         a, b, s = OWN[n]
         if s == 3 and not topo.mates(topo.chip(core), topo.chip(peer(-s))):
             wait("G", *[t for t in f_tok[2] if b > OWN[1][1] or t[0] != "af2"])
@@ -448,7 +488,7 @@ def rank_program(g, core, T, topo):
             sent += hand_on(g, core, T, topo, rank, a, b, s)
     total["sent"] = sent
 
-    for q, out, src in (("SY", "yc", T.oc), ("S", "yf", T.of), ("SY", "yp", T.op)):
+    for q, out, src in (("SY", "yf", T.of), ("SY", "yp", T.op), ("S", "yc", T.oc)):
         wait(q, *[(out + "_" + str(h), 1) for h in range(NH)])
         inc(Qs[q].dma_start(T[out][:], src[:]), "sty", 16)
     waited = {}

from concourse.mybir import dt, AluOpType, AxisListType, ActivationFunctionType

ALU = AluOpType
ACT = ActivationFunctionType
P, Q, K = 4096, 1024, 64
CUT = (0, 32, 64)
NH = len(CUT) - 1
W = max(b - a for a, b in zip(CUT, CUT[1:]))
NN = 4 * NH
J = 2 * K
MID, BIG = 1800, 4096.0
HALF = "float16"
GUEST = 1
SLOT = (0, 0, 1, 2)
ROUTES = ["VVMM"] * 4 + ["VVMS"] * 3 + ["VVMM"]
POS = (0, 2, 1, 3)

OWN = ((-J, 640, 2), (640, 1664, 2), (-J, 896, 3), (896, 2176, 3))
FEEDS = ((1664, 2176, 0), (2176, 2816, 1), (3392, P, 0), (2816, 3392, 1))
HELP = [[(a, b, s) for s in (2, 3) for a, b, x in FEEDS if x == h and (s == 2 or a >= OWN[3][1])] for h in range(2)]

AWAY = {"V": [("g0", 0), ("g1", 0), ("s2", 0), ("t2", 0), ("s3", 0), ("t3", 0), ("xy", 1), ("px", 1), ("cv", 1), ("pu", 1),
              ("m1", 0), ("m2", 0), ("off", 1), ("m3", 0), ("of2", 1), ("m4", 0), ("g0", 1), ("plc", 1)],
        "S": [("g2", 0), ("g3", 0), ("s0", 0), ("t0", 0), ("s1", 0), ("t1", 0), ("kc", 0)],
        "PE": [("a2", 0), ("a3", 0), ("b2", 0), ("pre", 0), ("b3", 0), ("a2", 1), ("ke", 0), ("kf", 0), ("kl", 0), ("km", 0),
               ("cc", 1), ("cd", 1), ("a3", 1)]}
FIRST = {"V": AWAY["V"][:6] + [("g0", 1), ("m1", 0), ("m2", 0), ("m3", 0), ("nk", 1), ("m4", 0)],
         "S": AWAY["S"][:-1] + [("us", 1), ("kc", 0)], "PE": AWAY["PE"][:-1] + [("nu", 1), ("a3", 1)]}
HOME = {"V": [("g0", 0), ("m1", -1), ("of2", 0), ("q2", -1), ("m2", -1), ("plc", 0), ("g1", 0), ("m3", -1), ("s2", 0),
              ("m4", -1), ("t2", 0), ("xy", 1), ("px", 1), ("q0", 0), ("cv", 1), ("pu", 1), ("q1", 0), ("off", 1)],
        "S": [("g2", 0), ("g3", 0), ("s0", 0), ("t0", 0), ("s1", 0), ("t1", 0), ("s3", 0), ("t3", 0), ("kc", 0)],
        "PE": [("a3", 0), ("b2", 0), ("pre", 0), ("a2", 1), ("b3", 0), ("ke", 0), ("kf", 0), ("cc", 1), ("cd", 1),
               ("kl", 0), ("km", 0)]}
LAST = dict(HOME, V=[("g0", 0), ("of2", 0), ("m1", -1), ("q2", -1), ("plc", 0), ("g1", 0), ("m2", -1), ("s2", 0), ("m3", -1),
                     ("t2", 0), ("s3", 0), ("m4", -1), ("t3", 0), ("q0", 0), ("q1", 0), ("q2", 0), ("m1", 0), ("m2", 0),
                     ("z0", 0), ("m3", 0), ("z1", 0), ("z2", 0), ("z3", 0), ("z4", 0)])

SCRATCH = {
    "fa": ("sbuf", [128, 3, J + P], "bfloat16"),
    "ua": ("sbuf", [128, 2, Q], "bfloat16"), "usq": ("sbuf", [128, Q], "bfloat16"),
    "nq": ("sbuf", [128, 2, NH * 2 * W], HALF),
    "jraw": ("sbuf", [128, K], "int32"), "jint": ("sbuf", [128, 2 * K], "int32"),
    "mo": ("sbuf", [128, 5, K], "int32"), "mg": ("sbuf", [128, 2, K], "int32"),
    "xyi": ("sbuf", [128, 4, 3, K], "int32"), "xyb": ("sbuf", [128, 16, K + 2], "bfloat16"),
    "off": ("sbuf", [128, NN, 4 * W], "uint16"), "plc": ("sbuf", [128, NN, 4 * W], HALF),
    "gd": ("sbuf", [128, NN, 64 * W], "bfloat16"), "sq": ("sbuf", [128, NN, 64 * W], "bfloat16"),
    "kec": ("sbuf", [128, NN, 2 * W], "float32"), "ab": ("sbuf", [128, NN, 2 * W], "int32"),
    "abc": ("sbuf", [128, NN, 2 * W], "int32"), "bs": ("sbuf", [128, NN, W], "int32"),
    "ones": ("sbuf", [128, 128], "bfloat16"), "eye": ("sbuf", [128, 128], "bfloat16"), "eye64": ("sbuf", [128, 128], "bfloat16"),
    "eyem": ("sbuf", [128, 2, 128], "bfloat16"), "sh": ("sbuf", [128, 2, 128], "bfloat16"), "wr": ("sbuf", [128, 2, 128], "bfloat16"),
    "eyeh": ("sbuf", [128, 128], HALF), "eyek": ("sbuf", [128, 128], HALF),
    "cl": ("sbuf", [128, 128], "bfloat16"), "ct": ("sbuf", [128, 2 * NH, 2, 2 * W], "bfloat16"),
    "blk": ("sbuf", [128, 16], "bfloat16"), "sel": ("sbuf", [128, 144], "bfloat16"),
    "pen": ("sbuf", [128, 16], "float32"),
    "ti": ("sbuf", [128, 16, K], "int32"), "tf": ("sbuf", [128, 8, K], "float32"),
    "oc": ("sbuf", [128, K], "float32"), "of": ("sbuf", [128, K], "float32"), "op": ("sbuf", [128, K], "float32"),
}
for _h in range(2):
    for _n in ("pa", "pb", "pc", "pl"):
        SCRATCH[_n + str(_h)] = ("psum", [128, 512], "float32")
KE = 256

ROLES = {"xy": 2, "cv": 2, "cc": 1, "cd": 1, "off": 1, "of2": 1, "plc": 1, "g0": 1, "g1": 1, "g2": 1, "g3": 1,
         "s0": 1, "s1": 1, "s2": 1, "s3": 1, "t0": 1, "t1": 1, "t2": 1, "t3": 1, "px": 1, "pu": 1, "b2": 1, "b3": 1,
         "kf": 1, "km": 1, "kc": 1, "m1": 1, "m2": 1, "m3": 1, "m4": 1}
FIN = {"fn": 1, "fk": 1, "fc": 1, "fp": 2, "ff": 1, "yc": 1, "yp": 1, "yf": 1}
SEMAPHORES = ([r + "_" + str(h) for r in list(ROLES) + list(FIN) for h in range(NH)]
              + ["hp%d" % k for k in range(len(FEEDS))] + [a + str(h) for a in ("ldu", "us", "nu", "nk", "au") for h in range(NH)]
              + ["arr%d" % n for n in range(NH, 3 * NH)] + [a + str(k) for a in ("af", "aj") for k in (2, 3)]
              + [a + str(k) for a in "tc" for k in range(12)]
              + ["ldf", "lds", "ldj", "sty", "sent", "j0", "j1", "an", "ag"])


def mask_of(engs):
    m = 0
    for e in engs:
        m |= 1 << e
    return m


def helpers_of(T, topo, rank):
    me = T.cores[rank]
    return sorted([x for x in topo.cores_of(me) if x != me and all(topo.may_write(x, c) for c in T.cores)],
                  key=lambda x: topo.die(x) == topo.die(me))


def near_engines(T, topo, rank):
    me = T.cores[rank]
    return [e for e in topo.engines(me, helpers_of(T, topo, rank)[0]) if e not in topo.engines(me, T.cores[rank - 1])]


def write(g, T, topo, dst, out, in_, sem, engs):
    rid, pid, _ = topo.addr(dst)
    g.remote_dma(out, in_, T.sem[sem], T.sem.sent, pid, rid, mask_of(engs))
    return len(engs)


def hand_on(g, core, T, topo, rank, a, b, s, slot=0):
    dst = T.cores[rank - s]
    return write(g, T, topo, dst, T.fa[:, SLOT[s], J + a:J + b], T.fa[:, slot, J + a:J + b], landed(a, b, s), topo.engines(core, dst))


def landed(a, b, s):
    return "aj%d" % s if a < 0 else "ag" if (a, b, s) == OWN[1] else "af%d" % s


def helper_program(g, core, T, topo, rank, h):
    sent, here = 0, []
    for a, b, s in HELP[h]:
        k = FEEDS.index((a, b, h))
        if k not in here:
            here.append(k)
            g.wait_ge(T.sem["hp%d" % k], len(near_engines(T, topo, rank)))
        sent += hand_on(g, core, T, topo, rank, a, b, s)
    g.wait_ge(T.sem.sent, sent)


def rank_program(g, core, T, topo):
    rank = T.rank_of(core)
    nr = len(T.cores)
    if rank is None:
        for r in range(nr):
            hs = helpers_of(T, topo, r)[:len(HELP)]
            if core in hs:
                helper_program(g, core, T, topo, r, hs.index(core))
        return
    V, S, PE, SY = g.vector, g.scalar, g.tensor, g.sync
    Qs = {"V": V, "S": S, "PE": PE, "SY": SY, "G": g}
    seen = {k: {} for k in Qs}
    total = {}

    def wait(q, *toks):
        for name, val in toks:
            if seen[q].get(name, 0) < val:
                Qs[q].wait_ge(T.sem[name], val)
                seen[q][name] = val

    def inc(ins, name, k=1):
        ins.then_inc(T.sem[name], k)
        total[name] = total.get(name, 0) + k

    home = lambda n: n >= (GUEST + 1) * NH
    has = lambda role, n: home(n) or role not in ("px", "pu") and role[0] != "q"

    def tok(role, n):
        return (role + "_" + str(n % NH), ROLES[role] * len([m for m in range(n % NH, n + 1, NH) if has(role, m)]))

    def rinc(ins, role, n):
        inc(ins, role + "_" + str(n % NH))

    peer = lambda d: T.cores[(rank + d) % nr]
    NE = len(topo.engines(core, peer(1)))

    inc(S.dma_start(T.mo[:, 0, :], T.st[:]), "lds", 16)
    inc(S.dma_start(T.jraw[:], T.ju[:]), "ldj", 16)
    for h in range(NH):
        inc(SY.dma_start(T.ua[:, 0, 16 * CUT[h]:16 * CUT[h + 1]], T.qu[:, 16 * CUT[h]:16 * CUT[h + 1]]), "ldu%d" % h, 16)
        if h == 0:
            inc(SY.dma_start(T.fa[:, 0, J:J + P], T.fr[:]), "ldf", 16)

    inc(V.memset(T.ones[:], 1.0), "c0")
    inc(V.memset(T.wr[:], 0.0), "c1")
    inc(V.memset(T.sel[:], 0.0), "c1")
    inc(V.memset(T.sh[:, :, 0:1], 0.0), "c1")
    inc(V.memset(T.xyb[:, :, 0:2], 0.0), "c1")
    inc(V.memset(T.cl[:], 0.0), "c10")
    inc(V.memset(T.ct[:], 0.0), "c10")
    inc(V.memset(T.nq[:, 0, :], -float(MID)), "c10")
    wait("G", ("c0", 1))
    inc(g.affine_select(T.eye[:], T.ones[:], [[-1, 128]], ALU.is_equal, 0.0, 0, 1), "c2")
    inc(g.affine_select(T.blk[:, 0:8], T.ones[:, 0:8], [[-16, 8]], ALU.is_ge, 0.0, 0, 1), "c8")
    wait("G", ("c8", 1))
    inc(g.affine_select(T.blk[:, 8:16], T.blk[:, 0:8], [[16, 8]], ALU.is_ge, 0.0, 15, -1), "c3")
    wait("S", ("c2", 1))
    inc(S.activation(T.eye64[:], T.eye[:], ACT.Copy, scale=64.0), "c6")
    inc(S.activation(T.eyem[:, 0, :], T.eye[:], ACT.Copy, scale=-1.0), "c6")
    inc(S.activation(T.eyem[:, 1, :], T.eye[:], ACT.Copy, scale=-2.0), "c6")
    wait("V", ("c10", 3))
    inc(V.memset(T.cl[0:1, :], 8192.0), "c7")
    inc(V.memset(T.cl[32:33, :], 2048.0), "c7")
    inc(V.memset(T.cl[64:65, 0:128:16], 8192.0), "c7")
    inc(V.memset(T.ct[0:1, NH:2 * NH, :, :], -float(MID)), "c11")
    inc(V.memset(T.ct[32:33, :, 0, :], 1.0), "c7")
    inc(V.memset(T.ct[32:33, :, 1, :], 3.0), "c7")
    for h in range(NH):
        inc(V.memset(T.ct[64:65, h:2 * NH:NH, 1, 0:CUT[h + 1] - CUT[h]:2], BIG), "c7")
    wait("V", ("c11", 1))
    inc(V.memset(T.ct[0:1, 0:2 * NH:NH, 0, CUT[1]:CUT[1] + 2], BIG), "c7")
    wait("V", ("c1", 4), ("c2", 1))
    inc(V.tensor_reduce(T.pen[:, 0:1], T.eye[:, 15:128:16], AxisListType.X, ALU.add), "c4")
    inc(V.tensor_copy(T.wr[:, 0, 0:128:16], T.eye[:, 15:128:16]), "c5")
    inc(V.tensor_scalar(T.wr[:, 1, 0:128:16], T.eye[:, 15:128:16], 64.0, None, ALU.mult), "c5")
    wait("V", ("c4", 1))
    inc(V.tensor_scalar(T.pen[:, 8:9], T.pen[:, 0:1], -1.0, 1.0, ALU.mult, ALU.add), "c9")
    inc(V.tensor_copy(T.eyeh[:], T.eye[:]), "c7")
    inc(V.tensor_scalar(T.eyek[:], T.eye[:], 8192.0, None, ALU.mult), "c7")
    wait("V", ("c3", 1))
    inc(V.tensor_scalar(T.sel[:, 15:143:16], T.blk[:, 8:16], 8192.0, None, ALU.mult), "c7")
    wait("V", ("c9", 1))
    inc(V.tensor_scalar(T.sh[:, 0, 1:128], T.eye[:, 0:127], T.pen[:, 8:9], None, ALU.mult), "c5")
    inc(V.tensor_scalar(T.sh[:, 1, 1:128], T.eye[:, 0:127], T.pen[:, 8:9], 64.0, ALU.mult, ALU.mult), "c5")
    wait("PE", ("c7", total["c7"]), ("c1", 4), ("c5", 4), ("c6", 3), ("c2", 1))

    far = [x for l in HELP for x in l] + list(OWN)
    own_f, own_j = [("ldf", 16)], [("j1", 1)]
    j_tok = [own_j, own_j] + [[("aj%d" % s, NE)] for s in (2, 3)]
    arrive = lambda s: [landed(*x) for x in far if x[2] == s]
    f_tok = [own_f, own_f] + [[(k, NE * arrive(s).count(k)) for k in sorted(set(arrive(s)))] for s in (2, 3)]
    u_tok = lambda n: ("au%d" % (n % NH), NE) if n // NH == GUEST else ("ldu%d" % (n % NH), 16)
    n_tok = lambda n: ("an", NE) if n // NH == GUEST else ("nk%d" % (n % NH), 1)
    span = lambda n: (n // NH, CUT[n % NH], CUT[n % NH + 1], CUT[n % NH + 1] - CUT[n % NH])
    ps = lambda name, n: T[name + str(n % 2)]
    k_in = lambda s, a, b: T.mg[:, 0, a:b] if s == GUEST else T.mo[:, s, a:b]
    k_out = lambda s, a, b: T.mg[:, 1, a:b] if s == GUEST else T.mo[:, s + 1, a:b]

    def there(n):
        s = n // NH
        return ("lds", 16) if s == 0 else ("arr%d" % n, NE) if s in (GUEST, GUEST + 1) else tok("m4", n - NH)

    fr = [float((rank + s) % nr) for s in range(4)]
    ti = lambda k: T.ti[:, k, :]
    tf = lambda k: T.tf[:, k, :]
    keys = lambda s: [there((s + 1) * NH + h) for h in range(NH)]

    def best(i, j):
        if (i, j) == (0, 0):
            wait("V", *keys(1))
            inc(V.tensor_scalar(T.ti[:, 0:2, :], T.mo[:, 1:3, :], -4097, None, ALU.bitwise_and), "t0")
        elif (i, j) == (0, 1):
            wait("V", ("t0", 1))
            inc(V.tensor_scalar(ti(2), ti(1), 4096.0, None, ALU.add), "t1")
        elif (i, j) == (0, 2):
            wait("V", ("t1", 1))
            inc(V.tensor_tensor(ti(3), ti(0), ti(2), ALU.min), "t2")
        elif (i, j) == (1, 0):
            wait("V", ("t2", 1))
            inc(V.tensor_scalar(ti(6), ti(3), 12, 1, ALU.arith_shift_right, ALU.bitwise_and), "t3")
            inc(V.tensor_scalar(ti(4), ti(3), -8192, None, ALU.bitwise_and), "t4")
        elif (i, j) == (1, 1):
            wait("V", ("t3", 1))
            inc(V.tensor_scalar(tf(0), ti(6), fr[1] - fr[0], fr[0] - fr[2], ALU.mult, ALU.add), "t4")
            inc(V.tensor_scalar(ti(5), ti(3), P - 1, None, ALU.bitwise_and), "t4")
        elif (i, j) == (2, 0):
            wait("V", ("t4", 3), *keys(2))
            inc(V.tensor_tensor(ti(7), T.mo[:, 3, :], ti(4), ALU.min), "t5")
            inc(V.tensor_tensor(tf(1), T.mo[:, 3, :], ti(4), ALU.is_ge), "t6")
        elif (i, j) == (2, 1):
            wait("V", ("t5", 1))
            inc(V.tensor_scalar(ti(8), ti(7), -8192, None, ALU.bitwise_and), "t8")
            inc(V.tensor_scalar(ti(10), ti(7), P - 1, None, ALU.bitwise_and), "t7")
            wait("V", ("t6", 1))
            inc(V.tensor_tensor(tf(2), tf(1), ti(5), ALU.mult), "t7")
            inc(V.tensor_tensor(tf(3), tf(1), tf(0), ALU.mult), "t7")
        elif (i, j) == (2, 2):
            wait("V", ("t7", 3))
            inc(V.tensor_tensor(ti(9), tf(2), ti(10), ALU.add), "t8")
            inc(V.tensor_scalar(tf(4), tf(3), fr[2] - fr[3], None, ALU.add), "t8")

    def results(n, j):
        s, a, b, w = span(n)
        ft = lambda role: (role + "_" + str(n % NH), FIN[role])
        m, thr, new, keep = T.mo[:, 4, a:b], T.ti[:, 8, a:b], T.ti[:, 13, a:b], T.tf[:, 5, a:b]
        if j == 0:
            wait("V", ("t8", 3), tok("m4", n))
            rinc(V.tensor_tensor(new, m, thr, ALU.min), "fn", n)
            rinc(V.tensor_tensor(keep, m, thr, ALU.is_ge), "fk", n)
        elif j == 1:
            wait("V", ft("fn"))
            rinc(V.tensor_scalar(T.ti[:, 14, a:b], new, 13, None, ALU.arith_shift_right), "fc", n)
            rinc(V.tensor_scalar(T.ti[:, 15, a:b], new, P - 1, None, ALU.bitwise_and), "fp", n)
            wait("V", ft("fk"))
            rinc(V.tensor_tensor(T.tf[:, 7, a:b], keep, T.tf[:, 4, a:b], ALU.mult), "ff", n)
            rinc(V.tensor_tensor(T.tf[:, 6, a:b], keep, T.ti[:, 9, a:b], ALU.mult), "fp", n)
        elif j == 2:
            wait("V", ft("fc"))
            rinc(V.tensor_scalar(T.oc[:, a:b], T.ti[:, 14, a:b], float(MID), None, ALU.add), "yc", n)
            wait("V", ft("ff"))
            rinc(V.tensor_scalar(T.of[:, a:b], T.tf[:, 7, a:b], fr[3], None, ALU.add), "yf", n)
            wait("V", ft("fp"))
            rinc(V.tensor_tensor(T.op[:, a:b], T.tf[:, 6, a:b], T.ti[:, 15, a:b], ALU.add), "yp", n)

    def last_results(n, j):
        s, a, b, w = span(n)
        ft = lambda role: (role + "_" + str(n % NH), FIN[role])
        thr, low, new, keep = T.ti[:, 8, a:b], T.ti[:, 12, a:b], T.ti[:, 13, a:b], T.tf[:, 5, a:b]
        if j == 0:
            wait("V", ("t8", 3), tok("m1", n))
            for k in range(2):
                inc(V.tensor_tensor(T.tf[:, k, a:b], T.ab[:, n, k * w:(k + 1) * w], thr, ALU.is_ge), "t9")
        elif j == 1:
            wait("V", tok("m2", n))
            inc(V.tensor_tensor(low, T.abc[:, n, 0:w], thr, ALU.min), "t10")
            wait("V", ("t9", 2))
            rinc(V.tensor_tensor(keep, T.tf[:, 0, a:b], T.tf[:, 1, a:b], ALU.mult), "fk", n)
        elif j == 2:
            wait("V", ("t10", 1), tok("m3", n))
            rinc(V.tensor_tensor(new, low, T.bs[:, n, 0:w], ALU.min), "fn", n)
            wait("V", ft("fk"))
            rinc(V.tensor_tensor(T.tf[:, 7, a:b], keep, T.tf[:, 4, a:b], ALU.mult), "ff", n)
            rinc(V.tensor_tensor(T.tf[:, 6, a:b], keep, T.ti[:, 9, a:b], ALU.mult), "fp", n)
        elif j == 3:
            wait("V", ft("fn"))
            rinc(V.tensor_scalar(T.ti[:, 15, a:b], new, P - 1, None, ALU.bitwise_and), "fp", n)
            rinc(V.tensor_scalar(T.ti[:, 14, a:b], new, 13, None, ALU.arith_shift_right), "fc", n)
            wait("V", ft("ff"))
            rinc(V.tensor_scalar(T.of[:, a:b], T.tf[:, 7, a:b], fr[3], None, ALU.add), "yf", n)
        else:
            wait("V", ft("fp"))
            rinc(V.tensor_tensor(T.op[:, a:b], T.tf[:, 6, a:b], T.ti[:, 15, a:b], ALU.add), "yp", n)
            wait("V", ft("fc"))
            rinc(V.tensor_scalar(T.oc[:, a:b], T.ti[:, 14, a:b], float(MID), None, ALU.add), "yc", n)

    def emit(e, stage, n):
        s, a, b, w = span(n)
        q = 16 * w
        u = T.ua[:, int(s == GUEST), 16 * a:16 * b]
        ke, kl = ps("pc", n)[:, KE:KE + 2 * w], ps("pl", n)[:, KE:KE + 2 * w]
        if stage == "us":
            wait("S", u_tok(n))
            inc(S.activation(T.usq[:, 16 * a:16 * b], u, ACT.Square), "us%d" % n)
            return
        if stage == "nu":
            wait("PE", ("us%d" % n, 1), tok("of2", n))
            for r in range(16):
                ins = PE.matmul(ps("pl", n)[:, 2 * w:3 * w], T.sel[:, 15 - r:143 - r], T.usq[:, 16 * a + r:16 * b:16], r == 0, r == 15)
            inc(ins, "nu%d" % n)
            return
        if stage == "nk":
            wait("V", ("nu%d" % n, 1))
            inc(V.tensor_scalar(T.nq[:, 0, 2 * a + w:2 * b], ps("pl", n)[:, 2 * w:3 * w], 1.0 / 8192, -float(MID), ALU.mult, ALU.add),
                "nk%d" % n)
            return
        if stage[0] in "gstab":
            c = int(stage[1])
            k, route = POS[c], ROUTES[n][c]
            lo, step = {"s": (0, 2), "t": (1, 2)}.get(stage[0], (0, 1))
            gd, sq = T.gd[:, n, k * q + lo:(k + 1) * q:step], T.sq[:, n, k * q + lo:(k + 1) * q:step]
            pb = ps("pb" if c == 3 else "pa", n)[:, lo:q:step]
        if stage == "xy":
            wait("V", there(n))
            rinc(V.tensor_scalar(T.xyi[:, s, 0, a:b], k_in(s, a, b), 63, None, ALU.bitwise_and), "xy", n)
            rinc(V.tensor_scalar(T.xyi[:, s, 1, a:b], k_in(s, a, b), 6, 63, ALU.arith_shift_right, ALU.bitwise_and), "xy", n)
        elif stage == "px":
            wait("V", there(n))
            rinc(V.tensor_scalar(T.xyi[:, s, 2, a:b], k_in(s, a, b), P - 1, None, ALU.bitwise_and), "px", n)
        elif stage == "pu":
            wait("V", tok("px", n))
            rinc(V.tensor_copy(T.off[:, n, 0:w], T.xyi[:, s, 2, a:b]), "pu", n)
        elif stage == "cv":
            wait("V", tok("xy", n), ("c1", 4))
            src = T.xyi[:, s, 0:2, a:b]
            rinc(V.tensor_copy(T.xyb[:, 4 * s:4 * s + 2, 2 + a:2 + b], src), "cv", n)
            rinc(V.tensor_scalar(T.xyb[:, 4 * s + 2:4 * s + 4, 2 + a:2 + b], src, 1.0, 63.0, ALU.add, ALU.min), "cv", n)
        elif stage in ("cc", "cd"):
            late = int(stage == "cd")
            wait("PE", tok("cv", n), tok("cv", n - 1), *([tok("m1", n - 2)] + j_tok[s] if late else [tok("kc", n - 2)]))
            pl = lambda k, d: T.xyb[:, 4 * s + k, 2 + a - d:2 + b - d]
            jp = lambda k: T.fa[:, SLOT[s], k * K + a:k * K + b]
            e1, e64 = T.eye[:], T.eye64[:]
            groups = [[(e64, pl(1, 0)), (e1, pl(0, 0))],
                      [(e64, pl(3, 2)), (e1, pl(0, 2))],
                      [(T.sh[:, 1, :], pl(1, 0)), (T.sh[:, 0, :], pl(2, 0)), (T.wr[:, 1, :], pl(1, 1)), (T.wr[:, 0, :], pl(2, 1))],
                      [(e64, pl(1, 0)), (e1, pl(0, 0)), (e64, jp(0)), (e1, jp(1))]]
            for k, grp in enumerate(groups[2 * late:2 * late + 2]):
                for j, (l, r) in enumerate(grp if late or k or not home(n) else ()):
                    ins = PE.matmul(ps(("pc", "pl")[late], n)[:, k * w:(k + 1) * w], l, r, j == 0, j == len(grp) - 1)
            rinc(ins, stage, n)
        elif stage in ("off", "of2"):
            late = int(stage == "of2")
            wait("V", tok(("cc", "cd")[late], n))
            lo = w if home(n) and not late else 0
            rinc(V.tensor_scalar(T.off[:, n, 2 * late * w + lo:2 * (late + 1) * w], ps(("pc", "pl")[late], n)[:, lo:2 * w],
                                 0.0, float(P - 1), ALU.max, ALU.min), stage, n)
        elif stage == "plc":
            wait("V", tok("off", n), tok("of2", n), tok("pu", n))
            rinc(V.tensor_scalar(T.plc[:, n, 0:4 * w], T.off[:, n, 0:4 * w], -2048.0, None, ALU.add), "plc", n)
        elif stage[0] == "g":
            win = T.fa[:, SLOT[s], J:J + P].indirect(T.off[:, n, k * w:(k + 1) * w])
            wait(e, tok("of2" if c % 2 else "pu" if c == 0 and home(n) else "off", n), *f_tok[s])
            if route == "V":
                wait(e, u_tok(n))
                rinc(V.tensor_tensor(gd, win, u, ALU.subtract), stage, n)
            else:
                rinc(S.activation(gd, win, ACT.Copy), stage, n)
        elif stage[0] == "a":
            wait("PE", u_tok(n), tok("s%d" % c, n - 2), tok("t%d" % c, n - 2))
            PE.matmul(pb, T.eyem[:, int(route == "M"), :], u, True, False)
        elif stage[0] == "b":
            wait("PE", tok("g%d" % c, n))
            rinc(PE.matmul(pb, T.eye[:], gd, False, True), stage, n)
        elif stage[0] in "st":
            wait(e, tok(("g%d" if route == "V" else "b%d") % c, n))
            if route == "M":
                rinc(V.tensor_tensor(sq, pb, gd, ALU.mult), stage, n)
            else:
                rinc(S.activation(sq, gd if route == "V" else pb, ACT.Square), stage, n)
        elif stage == "pre":
            wait("PE", tok("plc", n), n_tok(n))
            for j, kk in enumerate((ke, kl)):
                table = ROUTES[n][2 + j] == "M"
                PE.matmul(kk, T.eyeh[:], T.plc[:, n, 2 * j * w:2 * (j + 1) * w], True, False)
                PE.matmul(kk, T.cl[0:65, :], T.ct[0:65, n % NH + (0 if table else NH), j, 0:2 * w], False, False)
                if table:
                    PE.matmul(kk, T.eyek[:], T.nq[:, int(s == GUEST), 2 * a:2 * b], False, False)
        elif stage in ("ke", "kf", "kl", "km"):
            j, odd = int(stage in ("kl", "km")), int(stage in ("kf", "km"))
            wait("PE", tok("st"[odd] + str(j), n), tok("st"[odd] + str(2 + j), n))
            for r in range(odd, 16, 2):
                ins = PE.matmul((ke, kl)[j], T.sel[:, 15 - r:143 - r], T.sq[:, n, 2 * j * q + r:2 * (j + 1) * q:16], False, r == 15)
            if odd:
                rinc(ins, stage, n)
        elif stage == "kc":
            wait("S", tok("kf", n))
            rinc(S.activation(T.kec[:, n, 0:2 * w], ke, ACT.Copy), "kc", n)
        elif stage == "m1":
            wait("V", tok("kc", n), tok("km", n))
            rinc(V.tensor_tensor(T.ab[:, n, 0:2 * w], kl, T.kec[:, n, 0:2 * w], ALU.min), "m1", n)
        elif stage == "m2":
            wait("V", tok("m1", n))
            rinc(V.tensor_scalar(T.abc[:, n, 0:2 * w], T.ab[:, n, 0:2 * w], -4097, None, ALU.bitwise_and), "m2", n)
        elif stage == "m3":
            wait("V", tok("m2", n))
            rinc(V.tensor_scalar(T.bs[:, n, 0:w], T.abc[:, n, w:2 * w], 4096.0, None, ALU.add), "m3", n)
        elif stage == "m4":
            wait("V", tok("m3", n))
            rinc(V.tensor_tensor(k_out(s, a, b), T.abc[:, n, 0:w], T.bs[:, n, 0:w], ALU.min), "m4", n)
        elif stage[0] == "q" and n < NN - 1:
            best(n - 2 * NH, int(stage[1]))
        elif stage[0] == "q":
            results(n - 1, int(stage[1]))
        elif stage[0] == "z":
            last_results(n, int(stage[1]))

    def runs_on(e, stage, n):
        return stage[0] not in "st" or (e == "V") == (ROUTES[n][int(stage[1])] == "M")

    for n in range(NH):
        emit("V", "xy", n)
    wait("V", ("ldj", 16))
    inc(V.tensor_scalar(T.jint[:, 0:K], T.jraw[:], 6, None, ALU.arith_shift_right), "j0")
    inc(V.tensor_scalar(T.jint[:, K:2 * K], T.jraw[:], 63, None, ALU.bitwise_and), "j0")
    for n in range(NH):
        emit("V", "cv", n)
    wait("V", ("j0", 2))
    inc(V.tensor_copy(T.fa[:, 0, 0:J], T.jint[:]), "j1")
    for e, stages in (("PE", ("cc", "cd")), ("V", ("off", "of2"))):
        for n in range(NH):
            for stage in stages:
                emit(e, stage, n)
    for n in range(NH):
        emit("V", "plc", n)
    for e, stage in (("S", "us"), ("PE", "nu"), ("V", "nk")):
        emit(e, stage, 0)

    done = [(stage, n) for stage in ("xy", "cv", "cc", "cd", "off", "of2", "plc") for n in range(NH)]
    for e in ("V", "S", "PE"):
        for i in range(NN):
            for stage, d in (LAST if i == NN - 1 else HOME if home(i) else AWAY if i else FIRST)[e]:
                if 0 <= i + d < NN and (stage, i + d) not in done and runs_on(e, stage, i + d) and has(stage, i + d):
                    done.append((stage, i + d))
                    emit(e, stage, i + d)

    hs, near = helpers_of(T, topo, rank), near_engines(T, topo, rank)
    queries = lambda h: write(g, T, topo, peer(1), T.ua[:, 1, 16 * CUT[h]:16 * CUT[h + 1]],
                              T.ua[:, 0, 16 * CUT[h]:16 * CUT[h + 1]], "au%d" % h, topo.engines(core, peer(1)))
    wait("G", u_tok(0))
    sent = queries(0)
    wait("G", *own_f, *own_j)
    sent += hand_on(g, core, T, topo, rank, *OWN[0])
    for k, (a, b, h) in enumerate(FEEDS):
        part = T.fa[:, 0, J + a:J + b]
        sent += write(g, T, topo, hs[h], part, part, "hp%d" % k, near)
    for n in range((GUEST + 1) * NH):
        s, a, b, w = span(n)
        dst = peer(-1 if s == GUEST else 1)
        wait("G", tok("m4", n))
        sent += write(g, T, topo, dst, k_in(s + 1, a, b), k_out(s, a, b), "arr%d" % (n + NH), topo.engines(core, dst))
        if n == 0:
            wait("G", ("c10", 3), u_tok(1), *[n_tok(h) for h in range(NH)])
            sent += write(g, T, topo, peer(1), T.nq[:, 1, :], T.nq[:, 0, :], "an", topo.engines(core, peer(1)))
            sent += queries(1)
            continue
        a, b, s = OWN[n]
        if s == 3 and not topo.mates(topo.chip(core), topo.chip(peer(-s))):
            wait("G", *[t for t in f_tok[2] if b > OWN[1][1] or t[0] != "af2"])
            sent += hand_on(g, core, T, topo, (rank + 2) % nr, a, b, s, SLOT[2])
        else:
            sent += hand_on(g, core, T, topo, rank, a, b, s)
    total["sent"] = sent

    for q, out, src in (("SY", "yf", T.of), ("SY", "yp", T.op), ("S", "yc", T.oc)):
        wait(q, *[(out + "_" + str(h), 1) for h in range(NH)])
        inc(Qs[q].dma_start(T[out][:], src[:]), "sty", 16)
    waited = {}
    for q in seen:
        for k, v in seen[q].items():
            waited[k] = max(waited.get(k, 0), v)
    wait("G", *[(k, v) for k, v in total.items() if waited.get(k, 0) < v])
